import numpy as np, ml_dtypes
CORES = [40,41,42,43,44,45,46,47]
N = 8
import mx_ref
BF = ml_dtypes.bfloat16
def entries(a):
    return np.ascontiguousarray(a.T).reshape(-1)
def table(e):
    return np.ascontiguousarray(np.reshape(e, (-1, 16)).T).astype(np.int32)
def gcols(t, e):
    v = np.concatenate([t.reshape(8, 16, -1, 4), np.zeros((8, 16, 1, 4), BF)], axis=2)
    return np.ascontiguousarray(np.stack([v[g][:, e[g]] for g in range(8)])).reshape(128, -1)
def gpick(z, e):
    return np.concatenate([z[16 * g:16 * g + 16][:, e[g]] for g in range(8)])
def tile(rs):
    return np.stack(rs, axis=2).reshape(128, -1).astype(BF)
def pick(q, e):
    c = np.concatenate([q[0].reshape(128, -1, 4), np.zeros((128, 1, 4), np.uint8)], axis=1); s = np.concatenate([q[1], np.ones((16, 1), np.uint8)], axis=1)
    return (np.ascontiguousarray(c[:, e].reshape(128, -1)), np.ascontiguousarray(s[:, e]))
def join(*qs):
    return (np.concatenate([q[0] for q in qs], axis=1), np.concatenate([q[1] for q in qs], axis=1))
def put(q, e, v):
    c, s = q[0].reshape(128, -1, 4).copy(), q[1].copy(); c[:, e] = v[0].reshape(128, -1, 4); s[:, e] = v[1]
    return (c.reshape(128, -1), s)
def pk(c, s):
    return (np.ascontiguousarray(c), mx_ref.live(s))
def emit(q):
    return q[0], q[1]
def packed(v, rng):
    q = [mx_ref.quantize(np.ascontiguousarray(v[r])) for r in range(N)]
    return np.stack([a for a, b in q]), np.stack([mx_ref.plane(b, rng) for a, b in q])
def values_of_codes():
    e, c = np.zeros((128, 128, 4), np.float32), np.zeros((128, 2, 4), np.uint8)
    e[np.arange(128), np.arange(128), 0] = 1
    c[:127, :, 0] = np.arange(256).reshape(2, 128).T[:127]
    return mx_ref.matmul(mx_ref.quantize(e.reshape(128, 512).astype(BF)), (c.reshape(128, 8), np.full((16, 2), 127, np.uint8))).T.reshape(-1).astype(np.float64)
CODE_VALUE, SCALE_VALUE = values_of_codes(), 2.0 ** (np.arange(256) - 127.0)
def decode(q):
    return (CODE_VALUE[q[0]].reshape(16, 8, -1, 4) * SCALE_VALUE[q[1]][:, None, :, None] + 0.0).reshape(128, -1).astype(np.float32)
def f(rng, *shape):
    return mx_ref.flush((rng.standard_normal(shape, dtype=np.float32) * np.exp2(rng.integers(-2, 3, shape[:-1] + (1,)))).astype(BF))
def wide(rng, *shape, cols=0):
    v = rng.standard_normal(shape, dtype=np.float32) * np.exp2(rng.integers(-12, 13, shape)).astype(np.float32)
    if cols: v *= np.repeat(np.exp2(rng.integers(-cols, cols + 1, shape[:-2] + (1, shape[-1] // 4))) * (rng.random(shape[:-2] + (1, shape[-1] // 4)) > 0.0625), 4, axis=-1).astype(np.float32)
    return mx_ref.flush(v.astype(BF))
C, H, R = 384, 192, 3
WIDTH = [1, 3, 6, 12, 24, 48, 96, 192]
def big(v):
    v = v.astype(np.float32)
    v[np.abs(v) < np.float32(2.0 ** -16)] = 0
    return v.astype(BF)
def numbers_of(rng):
    return {"x": big(f(rng, N, 128, 4 * C)), "u": np.array(f(rng, N, 128, 512)), "v": np.array(f(rng, N, 128, 512))}
def bases(rng):
    return np.stack([table(rng.permutation(C)) for r in range(N)])
def layers(rng):
    return big(f(rng, N, 128, 2048)).reshape(N, 8, 16, 4, 8, 16, 4)
def weights(rng, w):
    c, s = packed(np.ascontiguousarray(w).reshape(N, 128, 2048), rng)
    return {"wc": c, "ws": s}
def setup_inputs(rng):
    return {**numbers_of(rng), "p": bases(rng), **weights(rng, layers(rng))}
def setup_inputs_ties(rng):
    d = numbers_of(rng)
    p = bases(rng)
    o = rng.permutation(N)
    x = d["x"].astype(np.float32).reshape(N, 8, 16, C, 4)
    n = (N, 8, 8, C, 4)
    x[:, :, 8:] = (1.125 + 0.25 * rng.integers(0, 4, n)) * np.exp2(-1.0 * rng.integers(8, 15, n)) * rng.choice([-1.0, 1.0], n)
    x[:, :, 8, :, 0] = 1.96875
    x[:, :, :8] = 0
    u = d["u"].reshape(N, 128, 128, 4)
    u[:, :, ::16] = 0
    for r in range(N):
        if o[r] % 2 == 1: x[r, :, 0, :, 0] = rng.integers(0, 4, (8, C))
        else: x[r, :, 0, :, 0] = rng.integers(0, 7, (1, C)) + rng.integers(0, 2, (8, C))
        for h in range(0, 128, 16): u[r, h, h, 0] = 0.0 if o[r] == 0 else -1.0 if o[r] == 1 else 1.0
        if o[r] == 0:
            x[r, 7, 0, :, 0] = 0
            x[r, 7, 0, p[r, 0, 0], 0] = 1
            u[r, 112, 112, 0] = 1.0
    w = layers(rng)
    w[:, :, :, :, :, :8] = 0
    return {"x": x.reshape(N, 128, 4 * C).astype(BF), "u": u.reshape(N, 128, 512), "v": d["v"], "p": p, **weights(rng, w)}
def setup_inputs_near(rng):
    d = numbers_of(rng)
    x = d["x"].astype(np.float32).reshape(N, 8, 16, C, 4)
    u = d["u"].reshape(N, 128, 128, 4)
    o = rng.permutation(N) % 4
    x[:, :, 0] = 0
    x[:, :, 8:] = 0
    u[:, :, ::16] = 0
    for r in range(N):
        k = 1.0 if o[r] == 0 else 2.0 ** -30
        if o[r] < 3:
            s = rng.integers(0, 252, (1, C)) + rng.integers(0, 4, (8, C))
            for i in range(2): x[r, :, 8 + i] = ((s[:, :, None] >> (4 * i + np.arange(4))) & 1) * np.exp2(4 * i + np.arange(4) - 23.0)
            if o[r] < 2:
                x[r, :, 0, :, 0] = rng.choice([-1.0, 1.0], C)
                x[r, :, 11, :, 0] = 2.0 ** -10
            for g in rng.permutation(8)[:4]: x[r, g, 0, rng.integers(C), 0] = 2.0 ** 29 * rng.choice([-1.0, 1.0])
        else:
            for i in (10, 12): x[r, :, i, :, 0] = (1.0 + 0.125 * rng.integers(0, 2, (8, C))) * 2.0 ** -30
        for h in range(0, 128, 16):
            if o[r] < 3:
                u[r, h, h, 0] = k
                u[r, h + 8:h + 10, h] = k
                u[r, h + 11, h, 0] = k
            else:
                a = rng.choice([-1.0, 1.0])
                u[r, h + 10, h, 0] = 1.125 * k * a
                u[r, h + 12, h, 0] = -k * a
    w = layers(rng)
    for i in (0, 8, 9, 10, 11, 12, 13, 14, 15):
        w[:, :, i] = 0
        w[:, :, :, :, :, i] = 0
    return {"x": x.reshape(N, 128, 4 * C).astype(BF), "u": u.reshape(N, 128, 512), "v": d["v"], "p": bases(rng), **weights(rng, w)}
def setup_inputs_huge(rng):
    d = numbers_of(rng)
    o = rng.permutation(N)
    x = 0.6 + 0.06 * rng.random((N, 8, 16, C, 4)) + 0.03 * rng.random((N, 1, 1, C, 1))
    a = 1.0 - 0.1 * rng.random((N, 128, 8, 4))
    for r in range(N):
        if o[r] < N // 2: a[r] *= -1.0
        else:
            x[r] *= rng.choice([-1.0, 1.0], (1, 1, C, 1))
            a[r] *= rng.choice([-1.0, 1.0], (1, 8, 1))
    u = d["u"].reshape(N, 128, 128, 4)
    u[:, :, ::16] = (2.0 ** 30 * a).astype(np.float32).astype(BF)
    w = np.zeros((N, 128, 4, 128, 4), np.float32)
    i = np.arange(128)
    for b in range(4): w[:, i, b, i, b] = -4
    return {"x": (2.0 ** 30 * x).astype(np.float32).reshape(N, 128, 4 * C).astype(BF), "u": u.reshape(N, 128, 512), "v": d["v"], "p": bases(rng), **weights(rng, w.astype(BF))}
def setup_inputs_ends(rng):
    v = np.array(f(rng, N, 128, 512))
    o = rng.permutation(N) % 4
    x, u = np.zeros((N, 128, C, 4), np.float32), np.zeros((N, 128, 128, 4), np.float32)
    w, e = np.zeros((N, 128, 4, 128, 4), np.float32), []
    i = np.arange(128)
    for r in range(N):
        c = rng.choice([-1.0, 1.0], (1, C, 1))
        a = rng.choice([-1.0, 1.0], (1, 128, 1))
        if o[r] == 0:
            x[r] = 2.0 ** 30
            x[r, 64:] *= rng.choice([0.5, 1.0], (64, C, 4))
            x[r, 64:, ::4] = 2.0 ** 30
            u[r] = -2.0 ** 30
            u[r, 64:, :64] = 0
        elif o[r] == 1:
            x[r] = 2.0 ** 30 * c
            u[r] = 2.0 ** 30 * a
        elif o[r] == 2:
            x[r] = 2.0 ** -29 * rng.choice([-1.0, 1.0], (128, C, 4))
            u[r] = 2.0 ** -30 * rng.choice([-1.0, 1.0], (128, 128, 4))
        else:
            x[r] = 2.0 ** -29 * c
            u[r] = 2.0 ** -30 * a
        if o[r] > 1:
            for b in range(4): w[r, i, b, i, b] = 2.0 ** -20
        e.append(table(np.arange(C) if o[r] % 2 == 0 else C - 1 - np.arange(C)))
    v = (np.where(v < 0, -1.0, 1.0) * np.where(rng.permutation(N) % 2, 2.0 ** -30, 2.0 ** 30)[:, None, None]).astype(np.float32).astype(BF)
    return {"x": x.reshape(N, 128, 4 * C).astype(BF), "u": u.reshape(N, 128, 512).astype(BF), "v": v, "p": np.stack(e), **weights(rng, w.astype(BF))}
def setup_inputs_spread(rng):
    d = setup_inputs(rng)
    d["x"] = big(wide(rng, N, 128, 4 * C, cols=6))
    return d
def check_inputs(d):
    bad = []
    for k in ("x", "u", "v"):
        a = np.abs(d[k].astype(np.float32))
        if not (np.isfinite(a).all() and ((a == 0) | (a >= 2.0 ** -30) & (a <= 2.0 ** 30)).all()): bad.append("a value of " + k)
    none, least, most = [emit(mx_ref.quantize(np.full((128, 16), k, np.float32).astype(BF)))[1][0, 0] for k in (0.0, 2.0 ** -30, 2.0 ** 30)]
    for r in range(N):
        if not np.array_equal(np.sort(d["p"][r].reshape(-1)), np.arange(C)): bad.append("p: not every column once")
        if ((d["wc"][r] == 0x7F) | (d["wc"][r] == 0xFF)).any(): bad.append("wc: a code that is no number")
        s = mx_ref.live(d["ws"][r])
        if ((s != none) & ((s < least) | (s > most))).any(): bad.append("ws: a scale out of range")
    return bad
def reference(x, u, v, p, wc, ws):
    qu = [mx_ref.quantize(u[r]) for r in range(N)]
    lay = [pk(wc[r], ws[r]) for r in range(N)]
    now = [x[r] for r in range(N)]
    base = [entries(p[r]) for r in range(N)]
    order = np.zeros((N, 8, C), np.int64)
    for t in range(R):
        own, sent = [], []
        for r in range(N):
            q = mx_ref.quantize(now[r])
            own.append(decode(q))
            s = mx_ref.matmul(qu[r], q)[::16] + np.float32(0.0)
            o = base[r]
            for g in range(8):
                key = np.maximum.accumulate(s[g][o].reshape(-1, WIDTH[g]), axis=1).reshape(-1, 2 * WIDTH[g])
                o = np.take_along_axis(o.reshape(-1, 2 * WIDTH[g]), np.argsort(key, axis=1, kind="stable"), axis=1).reshape(-1)
                order[r, g] = o
            base[r] = o
            a = own[r].astype(BF)
            z = (gcols(a, order[r, :, :H]).astype(np.float32) + gcols(a, order[r, :, H:]).astype(np.float32)) * np.float32(0.5)
            sent.append(mx_ref.quantize(z.astype(BF)))
        for r in range(N):
            q = sent[(r - 1) % N]
            place = np.argsort(order[r], axis=1) % H
            now[r] = tile([gpick(mx_ref.matmul(pick(lay[r], np.arange(128 * b, 128 * b + 128)), q), place) * np.float32(0.03125) + own[r][:, b::4] for b in range(4)])
    y, od = np.zeros((N, 128, C), np.float32), np.zeros((N, 8, C), np.float32)
    oc, osc = np.zeros((N, 128, 4 * C), np.uint8), np.zeros((N, 16, C), np.uint8)
    for r in range(N):
        q = mx_ref.quantize(now[r])
        y[r] = mx_ref.matmul(mx_ref.quantize(v[r]), q)
        od[r] = order[r]
        oc[r], osc[r] = emit(q)
    return {"y": y, "od": od, "oc": oc, "osc": osc}

@@ -1,0 +1,502 @@
+from concourse.mybir import dt, AluOpType as A, ActivationFunctionType as F_
+
+NR, H = 3, 192
+BIG = 1e29
+MAG = 201326592.0
+W = [1, 3, 6, 12, 24, 48, 96, 192]
+SCRATCH = {"ps": ("psum", [128, 4096], "float32")}
+ALIAS = {}
+for _d, _s in (
+    ("float32", "cc:64 bof:3 bxf:3 bdf:3 gx:96 dx:48 bb:48 own:48 dd:3 c7:579 pg:18 hm:18 ad:18 ldm:24 xm:24 x1:3 ow:24 h2:24 aj:24 iw:24 odf:384 odx:384 psb:768 g3:384 yb:384 sgb:3072 mk:48 a24f:24"),
+    ("bfloat16", "ioc:384 km:384 on:128 m4:147 m6:291 m7:579 idt:384 ea:2048 eb:2560 ut:512 vt:512 xt:1536 fb:1536 fh:1536 cm:147 c4:147 cm6:291 c6:291 cm7:579 tx5:512 tx6:512 tx7:512 bc:384 "
+                 "w1:768 t1:768 w2:768 t2:768 az:768 zt:768"),
+    ("int32", "pi:1 pw:16 bi:8 uli:64 a24:24 pin:24"),
+    ("uint16", "ul:64 stl:48 lp0:24 lbox:6 lbp:3 lb5:3 lb6:12 lb7:24 pl:4 plo:4 l6:12 l7:24 plu:24 lz:24 lj:24 lr:24"),
+    ("float8_e4m3fn_x4", "eac:512 ebc:640 uc:128 uqc:1024 vc:128 wq:512 xc:384 tc:128 zc0:192 zc1:192 zc2:192 lc0:192 lc1:192 lc2:192"),
+    ("uint8", "eas:512 ebs:640 us:128 uqs:1024 vs:128 wsc:512 xs:384 tsc:128 zs0:192 zs1:192 zs2:192 ls0:192 ls1:192 ls2:192"),
+):
+    for _w in _s.split():
+        SCRATCH[_w.split(":")[0]] = ("sbuf", [128, int(_w.split(":")[1])], _d)
+for _b, _s in (("kc", "fi:48 posr:48 aa:48 r2:48 r3:48 r4:48 r5:48 r6:192 r7:384 x8:16 mx4:16 mx8:16 pst:16 psl:16 tmp:144 om:384 bm:192"), ("sc", "sc1:48 sc2:48 sc3:48 sc4:48 sc5:48 sc5o:48 sc6:192 sc7:384"),
+               ("so", "so:48 so5:48 so6:192 so7:384"), ("key", "key:48 key5:48 key6:192 key7:384")):
+    _o = 0
+    for _w in _s.split():
+        ALIAS[_w.split(":")[0]] = (_b, _o)
+        _o += int(_w.split(":")[1])
+    SCRATCH[_b] = ("sbuf", [128, _o], "float32")
+SEMAPHORES = ["sv", "ss", "st", "sg", "ar0", "ar1", "ar2", "lsem", "dp", "dxin", "du", "dv", "dwc", "dws", "db5", "db6", "db7", "dl", "dbo", "dbx", "dout"]
+
+
+def rank_program(g, core, T, topo):
+    rank = T.rank_of(core)
+    if rank is None:
+        return
+    Q = {"v": g.vector, "s": g.scalar, "t": g.tensor, "g": g, "y": g.sync}
+    SEM = {"v": "sv", "s": "ss", "t": "st", "g": "sg"}
+    cnt, hist, dmh, acc = {}, {}, {}, {}
+    known = {e: {} for e in Q}
+    late, mode = [], {"defer": False, "mix": False}
+
+    def hit(r, q):
+        if r[2] <= q[1] or q[2] <= r[1] or r[5] <= q[4] or q[5] <= r[4]:
+            return False
+        return not (r[3] == q[3] and r[3] > 1 and (r[1] - q[1]) % r[3])
+
+    def need(e, sem, val):
+        k = known[e]
+        if k.get(sem, 0) >= val:
+            return
+        Q[e].wait_ge(T.sem[sem], val)
+        for s_, v_ in hist.get((sem, val), {}).items():
+            k[s_] = max(k.get(s_, 0), v_)
+        k[sem] = max(k.get(sem, 0), val)
+
+    def op(e, make, writes, reads, sem=None, pre=()):
+        if mode["defer"]:
+            late.append((e, make, writes, reads))
+            return
+        own = SEM.get(e) if sem is None else None
+        s = own if sem is None else sem
+        todo = {}
+        both = [(r, True) for r in writes] + [(r, False) for r in reads]
+        for r, wr in both:
+            bank = r[0] == "ps"
+            for q, qw, qs, qv in acc.get(r[0], []):
+                if bank and r[1] // 512 != q[1] // 512 or not bank and not hit(r, q) or not (wr or qw or bank):
+                    continue
+                if qs == own and (not hit(r, q) or not (wr or qw) or (e == "t" and wr)):
+                    continue
+                todo[qs] = max(todo.get(qs, 0), qv)
+        for a_, b_ in list(todo.items()) + list(pre):
+            need(e, a_, cnt[a_] if a_ in dmh else b_)
+        inc = 1 if sem is None else 16
+        make().then_inc(T.sem[s], inc)
+        cnt[s] = cnt.get(s, 0) + inc
+        h = dict(known[e])
+        if sem is not None:
+            old = dmh.setdefault(s, {})
+            for a_, b_ in h.items():
+                old[a_] = max(old.get(a_, 0), b_)
+            h = dict(old)
+        h[s] = cnt[s]
+        hist[(s, cnt[s])] = h
+        for r, wr in both:
+            keep = []
+            for x in acc.get(r[0], []):
+                q = x[0]
+                same = q == r and (wr or (not x[1] and x[2] == s))
+                if not (same or wr and r[3] == 1 and r[1] <= q[1] and q[2] <= r[2] and r[4] <= q[4] and q[5] <= r[5]):
+                    keep.append(x)
+            acc[r[0]] = keep + [(r, wr, s, cnt[s])]
+        if e == "v" and mode["mix"] and late:
+            mode["mix"] = False
+            op(*late.pop(0))
+            mode["mix"] = True
+
+    def P(name, a, b, st=1, p0=0, p1=128):
+        if name in ALIAS:
+            name, o = ALIAS[name]
+            a, b = a + o, b + o
+        t, c = T[name], slice(a, b) if st == 1 else slice(a, b, st)
+        ap = t[:, c] if (p0, p1) == (0, 128) else t[p0:p1, c]
+        return (ap, [(name, a, b, st, p0, p1)], [])
+
+    def IND(w, o):
+        return (w[0].indirect(o[0]), w[1], o[1])
+
+    def PS(bank, a, b, p0=0, p1=128):
+        return P("ps", 512 * bank + a, 512 * bank + b, 1, p0, p1)
+
+    def scl(s):
+        return (s[0], s[1]) if isinstance(s, tuple) else (s, [])
+
+    def tc(o, i):
+        op("v", lambda: g.vector.tensor_copy(o[0], i[0]), o[1], i[1] + i[2] + o[2])
+
+    def tt(o, i, j, k):
+        op("v", lambda: g.vector.tensor_tensor(o[0], i[0], j[0], k), o[1], i[1] + i[2] + j[1])
+
+    def ts(o, i, s1, s2, k1, k2=None):
+        (a, ra), (b, rb) = scl(s1), scl(s2)
+        op("v", lambda: g.vector.tensor_scalar(o[0], i[0], a, b, k1, k2) if k2 else g.vector.tensor_scalar(o[0], i[0], a, None, k1), o[1], i[1] + i[2] + ra + rb)
+
+    def scan(o, d0, d1, init, k0, k1):
+        op("v", lambda: g.vector.tensor_tensor_scan(o[0], d0[0], d1[0], init, k0, k1), o[1], d0[1] + d1[1])
+
+    def fill(o, c):
+        op("v", lambda: g.vector.memset(o[0], c), o[1], [])
+
+    def tr(o, i):
+        op("v", lambda: g.vector.transpose(o[0], i[0]), o[1], i[1])
+
+    def quant(c, s, i):
+        op("v", lambda: g.vector.quantize_mx(c[0], s[0], i[0]), c[1] + s[1], i[1])
+
+    def act(o, i, func=F_.Copy, bias=None, scale=None):
+        kw, rr = {}, []
+        for n, v in (("bias", bias), ("scale", scale)):
+            if v is not None:
+                kw[n], ra = scl(v)
+                rr = rr + ra
+        op("s", lambda: g.scalar.activation(o[0], i[0], func, **kw), o[1], i[1] + i[2] + rr)
+
+    def mm(o, l, ls, r, rs, start=True, stop=True, pre=()):
+        op("t", lambda: g.tensor.matmul_mx(o[0], l[0], ls[0], r[0], rs[0], start, stop), o[1], l[1] + ls[1] + r[1] + rs[1], pre=pre)
+
+    def dma(e, sem, o, i, wr, rd):
+        op(e, lambda: Q[e].dma_start(o, i), wr, rd, sem=sem)
+
+    def io(o, pat, base=0, cm=0, small=True):
+        op("g", lambda: g.iota(o[0], pat, base, cm, allow_small_or_imprecise_dtypes=True) if small else g.iota(o[0], pat, base, cm), o[1], [])
+
+    def sel(o, i, pat, cmp, base, cm):
+        op("g", lambda: g.affine_select(o[0], i[0], pat, cmp, 0.0, base, cm), o[1], i[1])
+
+    col = lambda k: P("cc", k, k + 1)
+    BFC, SGC, S29, SSC = 0, 8, 16, 22
+    PM, PM3, PM7, PM31, PMX, K6L, K7L, K5O, A6, A7, AF, Q96, O16, T0 = 30, 31, 32, 33, 34, 36, 37, 38, 40, 41, 42, 43, 44, 48
+    bit = lambda b: col(BFC + b)
+    sg = lambda k: col(SGC + k - 1)
+    TA, TB = col(T0 + 6), col(T0 + 7)
+
+    for q in range(8):
+        dma("y", "dp", T.pin[16 * q:16 * q + 16, :], T.p[:, :], P("pin", 0, 24, 1, 16 * q, 16 * q + 16)[1], [])
+    dma("s", "dxin", T.xt[:, :], T.x[:, :], P("xt", 0, 1536)[1], [])
+    dma("y", "du", T.ut[:, :], T.u[:, :], P("ut", 0, 512)[1], [])
+    io(P("pi", 0, 1), [[0, 1]], 0, 1, False)
+    io(P("uli", 0, 64), [[16, 8], [0, 8]], small=False)
+    io(P("fi", 0, 48), [[0, 3], [1, 16]])
+    io(P("posr", 0, 48), [[1, 48]])
+    io(P("ioc", 0, 384), [[1, 384]], -192)
+    io(P("x8", 0, 8), [[1, 8]])
+    io(P("pst", 0, 3), [[1, 3]], 0, 3)
+    io(P("a24", 0, 24), [[32, 24]], small=False)
+    ON, o6, o7 = P("on", 0, 128), P("idt", 128, 256), P("idt", 256, 384)
+    fill(ON, 1.0)
+    fill(P("ea", 0, 2048), 0.0)
+    for b in range(4):
+        sel(P("ea", 512 * b + b, 512 * b + 512, 4), ON, [[-1, 128]], A.is_equal, 0, 1)
+    sel(P("idt", 0, 128), ON, [[-32, 4], [16, 2], [-1, 16]], A.is_equal, -16, 1)
+    sel(o6, ON, [[-64, 2], [0, 4], [-4, 16]], A.is_ge, 0, 1)
+    sel(o6, o6, [[64, 2], [0, 4], [4, 16]], A.is_ge, 3, -1)
+    sel(o7, ON, [[0, 8], [-8, 16]], A.is_ge, 0, 1)
+    sel(o7, o7, [[0, 8], [8, 16]], A.is_ge, 7, -1)
+    io(P("km", 0, 384), [[0, 2], [1, 192]])
+    for b in range(7):
+        ts(P("bi", b, b + 1), P("pi", 0, 1), b, 1, A.logical_shift_right, A.bitwise_and)
+    for k, m in ((0, 15), (1, 3), (2, 7), (3, 31)):
+        ts(P("pw", k, k + 1), P("pi", 0, 1), m, None, A.bitwise_and)
+    for k in (1, 2, 3):
+        ts(P("pw", 4 + k, 5 + k), P("pw", 0, 1), k, None, A.logical_shift_right)
+    ts(P("pw", 8, 9), P("pi", 0, 1), 4, None, A.logical_shift_right)
+    tc(P("cc", BFC, BFC + 7), P("bi", 0, 7))
+    tc(P("cc", PM, PM + 4), P("pw", 0, 4))
+    tc(P("cc", T0, T0 + 4), P("pw", 5, 9))
+    tc(P("ul", 0, 64), P("uli", 0, 64))
+    ts(P("cc", SGC, SGC + 7), P("cc", BFC, BFC + 7), -2.0, 1.0, A.mult, A.add)
+    ts(P("cc", S29, S29 + 4), P("cc", SGC, SGC + 4), BIG, None, A.mult)
+    tt(P("cc", SSC, SSC + 6), P("cc", SGC, SGC + 6), P("cc", SGC + 1, SGC + 7), A.mult)
+
+    def base_out(e="odf", sem="dbo", to="bof", p=112):
+        dma("y", sem, T[to][:, :], T[e][p:p + 1, :], P(to, 0, 3)[1], P(e, 0, 384)[1])
+
+    tc(P("lp0", 0, 24), P("pin", 0, 24))
+    act(P("odf", 0, 384), IND(P("ioc", 0, 384), P("lp0", 0, 24)), F_.Identity, bias=192.0)
+    base_out()
+    tc(P("odx", 0, 384, 2), P("odf", 1, 384, 2))
+    tc(P("odx", 1, 384, 2), P("odf", 0, 384, 2))
+    base_out("odx", "dbx", "bxf")
+    dma("y", "dwc", T.wq[:, :].bitcast(dt.uint8), T.wc[:, :], P("wq", 0, 512)[1], [])
+    dma("y", "dws", T.wsc[:, :], T.ws[:, :], P("wsc", 0, 512)[1], [])
+    dma("y", "dv", T.vt[:, :], T.v[:, :], P("vt", 0, 512)[1], [])
+    uw, uo, ul = P("uc", 0, 128), P("uqc", 0, 1024), P("ul", 0, 64)
+    quant(uw, P("us", 0, 128), P("ut", 0, 512))
+    act(P("uqs", 0, 1024), IND(P("us", 0, 128), ul))
+    op("v", lambda: g.vector.tensor_copy(uo[0].bitcast(dt.uint32), uw[0].bitcast(dt.uint32).indirect(ul[0])), uo[1], uw[1] + ul[1])
+
+    def scores_in():
+        quant(P("xc", 0, 192), P("xs", 0, 192), P("xt", 0, 768))
+        quant(P("xc", 192, 384), P("xs", 192, 384), P("xt", 768, 1536))
+
+    def smm(gr, bank, a=0, b=384):
+        mm(PS(bank, 0, b - a), P("uqc", 128 * gr, 128 * gr + 128), P("uqs", 128 * gr, 128 * gr + 128), P("xc", a, b), P("xs", a, b))
+
+    def fmm(b, bank):
+        mm(PS(bank, 0, 384), P("eac", 128 * b, 128 * b + 128), P("eas", 128 * b, 128 * b + 128), P("xc", 0, 384), P("xs", 0, 384))
+
+    def xmm(k, bank, start=True, stop=True):
+        mm(PS(bank, 0, 128), P("ebc", 128 * k, 128 * k + 128), P("ebs", 128 * k, 128 * k + 128), P("tc", 0, 128), P("tsc", 0, 128), start, stop)
+
+    scores_in()
+    own = P("tmp", 0, 48)
+    ts(own, P("fi", 0, 48), col(PM), None, A.is_equal)
+    ts(P("aa", 0, 48), own, -1.0, 1.0, A.mult, A.add)
+    for t in range(3):
+        ts(P("om", 16 * t, 16 * t + 16), P("tmp", 16 * t, 16 * t + 16), sg(1), 1.0 if t != 1 else -1.0, A.mult, A.mult)
+    for k in range(1, 8):
+        ts(P("om", 48 * k, 48 * k + 48), own, sg(k), None, A.mult)
+    ts(TB, col(T0 + 3), -48.0, None, A.mult)
+    ts(P("pg", 0, 3), P("pst", 0, 3), TB, None, A.add)
+    ts(P("psl", 0, 3), P("pg", 0, 3), sg(1), None, A.mult)
+    ts(TA, col(PM), sg(1), None, A.add)
+    ts(P("tmp", 48, 96), P("fi", 0, 48), TA, None, A.is_equal)
+    ts(P("bm", 0, 48), P("tmp", 48, 96), 0.0, col(S29), A.is_equal, A.mult)
+    fill(P("r2", 0, 768), 0.0)
+    fill(P("m4", 0, 147), 1.0)
+    fill(P("m4", 0, 147, 49), 0.0)
+    mode["defer"] = True
+    for k in (2, 3, 4):
+        ts(TA, col(T0 + k - 2), sg(k), float(W[k]), A.add, A.mult)
+        ts(TB, TA, float(W[k]), None, A.add)
+        ts(P("tmp", 48, 96), P("posr", 0, 48), TA, None, A.is_ge)
+        ts(P("tmp", 96, 144), P("posr", 0, 48), TB, None, A.is_ge)
+        fill(P("r%d" % k, 0, 48, W[k]), -BIG)
+        tt(P("tmp", 48, 96), P("tmp", 48, 96), P("tmp", 96, 144), A.subtract)
+        ts(P("bm", 48 * k - 48, 48 * k), P("tmp", 48, 96), 0.0, col(S29 + k - 1), A.is_equal, A.mult)
+    quant(P("eac", 0, 512), P("eas", 0, 512), P("ea", 0, 2048))
+    for n in (5, 6, 7):
+        fill(P("r%d" % n, 0, 48 if n < 6 else 2 * W[n], W[n]), -BIG)
+    fill(P("eb", 0, 2560), 0.0)
+    for k, (src, a, b, wt) in enumerate(((0, 0, 128, 1.0), (128, 0, 128, 1.0), (256, 0, 128, 1.0), (256, 96, 112, 2.0), (256, 112, 128, 2.0))):
+        for d in range(2):
+            ts(P("eb", 512 * k + 4 * a + d, 512 * k + 4 * b, 4), P("idt", src + a, src + b), wt if d == 0 else 1.0, None, A.mult)
+    for n in ("tx5", "tx6", "tx7"):
+        fill(P(n, 0, 512), 0.0)
+    quant(P("ebc", 0, 512), P("ebs", 0, 512), P("eb", 0, 2048))
+    quant(P("ebc", 512, 640), P("ebs", 512, 640), P("eb", 2048, 2560))
+    for n, w in (("m6", 96), ("m7", 192)):
+        fill(P(n, 0, 3 * w + 3), 1.0)
+        fill(P(n, 0, 3 * w + 3, w + 1), 0.0)
+    ts(col(Q96), col(T0 + 3), 96.0, None, A.mult)
+    ts(col(O16), bit(4), 16.0, None, A.mult)
+    ts(TA, bit(4), 48.0, sg(6), A.mult, A.mult)
+    ts(TB, bit(5), 111.0, -103.5, A.mult, A.add)
+    ts(col(K6L), TA, TB, None, A.add)
+    ts(col(K5O), bit(4), 48.0, None, A.mult)
+    ts(TA, sg(4), sg(6), -48.0, A.mult, A.mult)
+    ts(TB, bit(2), 48.0, 48.0, A.mult, A.add)
+    ts(col(A6), TA, TB, None, A.add)
+    ts(P("mx4", 0, 4), P("x8", 0, 4), col(PM3), None, A.is_equal)
+    ts(P("mx8", 0, 8), P("x8", 0, 8), col(PM7), None, A.is_equal)
+    ts(TA, sg(7), 103.5, None, A.mult)
+    ts(TB, bit(6), 192.0, -192.0, A.mult, A.add)
+    ts(col(K7L), TA, TB, None, A.add)
+    ts(TA, sg(4), sg(7), -96.0, A.mult, A.mult)
+    ts(col(A7), TA, 199.5, None, A.add)
+    ts(TA, bit(3), 384.0, 199.5, A.mult, A.add)
+    ts(TB, bit(3), -384.0, 208.0, A.mult, A.add)
+    ts(col(AF), TB, bit(4), TA, A.mult, A.add)
+    fill(P("w1", 0, 768), 0.0)
+    tc(P("a24f", 0, 24), P("a24", 0, 24))
+    tt(col(PMX), col(PM31), sg(1), A.add)
+    ts(P("stl", 0, 24), P("a24f", 0, 24), col(PM31), None, A.add)
+    ts(P("stl", 24, 48), P("a24f", 0, 24), col(PMX), None, A.add)
+    mode["defer"], mode["mix"] = False, True
+
+    def flush(n):
+        while len(late) > n:
+            op(*late.pop(0))
+
+    SGR = lambda k: P("sgb", 384 * k, 384 * k + 384)
+    EX, FIN, BF3 = 4, 5, 6
+    nxt = T.cores[(rank + 1) % len(T.cores)]
+    rid, pid = topo.addr(nxt)[0], topo.addr(nxt)[1]
+    eng = topo.engines(core, nxt)
+    half = len(eng) // 2
+    mask_c, mask_s = sum(1 << e for e in eng[:half]), sum(1 << e for e in eng[half:])
+    ends = lambda cn, w: P(cn, w, 3 * w + 3, w + 1)
+    heads = lambda cn, w: P(cn, 0, 3 * w + 3, w + 1)
+
+    def keys(so, key, n, res, sc, lst):
+        tc(IND(P(so, 0, n), lst), P(sc, 0, n))
+        scan(P(key, 0, n), P(res, 0, n), P(so, 0, n), -BIG, A.add, A.max)
+
+    def owned(k, src):
+        tt(P("bb", 0, 48), src, P("om", 48 * k, 48 * k + 48), A.mult)
+        if k in (1, 2, 3, 4):
+            tt(P("mk", 0, 48), P("sc1" if k == 1 else "key", 0, 48), P("bm", 48 * k - 48, 48 * k), A.add)
+        scan(P("own", 0, 48), P("aa", 0, 48), P("bb", 0, 48), 0.0, A.mult, A.add)
+
+    def count(k, cmn, cn, mn, w, other):
+        for t in range(3):
+            ts(P(cmn, (w + 1) * t + 1, (w + 1) * t + w + 1), other, sg(k), P("own", 16 * t + 15, 16 * t + 16), A.mult, A.is_lt)
+        scan(P(cn, 0, 3 * w + 3), P(mn, 0, 3 * w + 3), P(cmn, 0, 3 * w + 3), 0.0, A.mult, A.add)
+
+    def lay(n, xs, tile):
+        for t in range(3):
+            ts(P("xm", t, 3 * n, 3), P("mx%d" % n, 0, n), xs[t], None, A.mult)
+        ts(P(tile, 0, 12 * n, 4), P("xm", 0, 3 * n), MAG, MAG, A.add, A.subtract)
+        tt(P(tile, 1, 12 * n, 4), P("xm", 0, 3 * n), P(tile, 0, 12 * n, 4), A.subtract)
+        quant(P("tc", 0, 128), P("tsc", 0, 128), P(tile, 0, 512))
+
+    pl, plo = P("pl", 0, 3), P("plo", 0, 3)
+    for r in range(NR):
+        last = r == NR - 1
+        if r:
+            scores_in()
+        smm(0, 0, 0, 192)
+        smm(0, 1, 192, 384)
+        smm(1, 2)
+        smm(2, 3)
+        tc(P("lbox", 0, 3), P("bof", 0, 3))
+        tc(P("lbox", 3, 6), P("bxf", 0, 3))
+        tt(P("bdf", 0, 3), P("bxf", 0, 3), P("bof", 0, 3), A.subtract)
+        tc(P("sgb", 0, 192), PS(0, 0, 192))
+        act(P("sgb", 192, 384), PS(1, 0, 192))
+        smm(3, 0)
+        smm(4, 1)
+        tc(P("gx", 0, 96), IND(SGR(0), P("lbox", 0, 6)))
+        tt(P("dx", 0, 48), P("gx", 0, 48), P("gx", 48, 96), A.subtract)
+        owned(0, P("dx", 0, 48))
+        ts(P("dd", 0, 3), P("own", 15, 48, 16), 0.0, None, A.is_gt)
+        for t in range(3):
+            ts(P("lbp", t, t + 1), P("dd", t, t + 1), P("bdf", t, t + 1), P("bof", t, t + 1), A.mult, A.add)
+        lp = P("lbp", 0, 3)
+        for name, n, src in (("lb5", 3, lambda q: (16 * (q + 1 - 2 * (q % 2)), 16)), ("lb6", 12, lambda q: (64 * (q // 4), 64)), ("lb7", 24, lambda q: (0, 128))):
+            for q in range(8):
+                a, m = src(q)
+                dma("y", "db" + name[2], T[name][16 * q:16 * q + 16, 0:n], T.lbp[a:a + m, 0:3], P(name, 0, n, 1, 16 * q, 16 * q + 16)[1], P("lbp", 0, 3, 1, a, a + m)[1])
+        for k in (1, 2):
+            act(SGR(k), PS(k + 1, 0, 384))
+            act(P("sc%d" % k, 0, 48), IND(SGR(k), lp))
+            if k == 1:
+                act(heads("cm", 48), P("psl", 0, 3))
+            smm(4 + k, k + 1)
+        tt(P("sc1", 16, 32), P("sc1", 16, 32), P("sc1", 0, 16), A.max)
+        tt(P("sc1", 32, 48), P("sc1", 32, 48), P("sc1", 16, 32), A.max)
+        owned(1, P("sc1", 0, 48))
+        count(1, "cm", "c4", "m4", 48, P("mk", 0, 48))
+        for k in (2, 3, 4):
+            ts(pl, ends("c4", 48), sg(k - 1), None, A.mult)
+            act(heads("cm", 48), ends("c4", 48), scale=col(SSC + k - 2))
+            act(P("pg", 3 * k - 3, 3 * k), ends("c4", 48), scale=sg(k - 1))
+            keys("so", "key", 48, "r%d" % k, "sc%d" % k, pl)
+            owned(k, IND(P("key", 0, 48), pl))
+            count(k, "cm", "c4", "m4", 48, P("mk", 0, 48))
+            act(SGR(k + 1), PS(k - 2, 0, 384))
+            act(P("sc%d" % (k + 1), 0, 48), IND(SGR(k + 1), lp))
+            if k == 2:
+                smm(7, 0)
+            elif k == 3:
+                fmm(0, 1)
+            else:
+                act(P("sc5o", 0, 48), IND(SGR(5), P("lb5", 0, 3)))
+        flush(23)
+        ts(P("tx5", 0, 12, 4), ends("c4", 48), MAG, MAG, A.add, A.subtract)
+        tt(P("tx5", 1, 12, 4), ends("c4", 48), P("tx5", 0, 12, 4), A.subtract)
+        quant(P("tc", 0, 128), P("tsc", 0, 128), P("tx5", 0, 512))
+        xmm(0, EX)
+        fmm(1, 2)
+        act(heads("cm", 48), ends("c4", 48), scale=col(SSC + 3))
+        act(P("pg", 12, 15), ends("c4", 48), scale=sg(4))
+        act(SGR(6), PS(3, 0, 384))
+        fmm(2, 3)
+        act(P("sc6", 0, 192), IND(SGR(6), P("lb6", 0, 12)))
+        act(P("fb", 0, 384), PS(1, 0, 384))
+        ts(pl, ends("c4", 48), sg(4), None, A.mult)
+        keys("so", "key", 48, "r5", "sc5", pl)
+        owned(5, IND(P("key", 0, 48), pl))
+        ts(plo, PS(EX, 0, 3), sg(4), None, A.mult)
+        keys("so5", "key5", 48, "r5", "sc5o", plo)
+        count(5, "cm", "c4", "m4", 48, P("key5", 0, 48))
+        flush(0)
+        lay(4, [P("c4", 49 * t + 48, 49 * t + 49) for t in range(3)], "tx6")
+        xmm(1, EX)
+        fmm(3, 1)
+        act(heads("cm6", 96), ends("c4", 48), F_.Identity, bias=col(K6L), scale=col(SSC + 4))
+        act(P("pg", 15, 18), ends("c4", 48), scale=sg(5))
+        act(SGR(7), PS(0, 0, 384))
+        act(P("sc7", 0, 384), IND(SGR(7), P("lb7", 0, 24)))
+        act(P("fb", 384, 768), PS(2, 0, 384))
+        ts(pl, ends("c4", 48), sg(5), col(K5O), A.mult, A.add)
+        a = 3 if r else 0
+        ts(P("hm", a, 18), P("pg", a, 18), -7.5, MAG, A.add, A.add)
+        ts(P("hm", a, 18), P("hm", a, 18), MAG, col(Q96), A.subtract, A.add)
+        tt(P("ad", a, 18), P("hm", a, 18), P("pg", a, 18), A.add)
+        for gr in range(a // 3, 6):
+            dma("y", "dl", T.ldm[16 * gr:16 * gr + 16, 0:24], T.ad[:, 3 * gr:3 * gr + 3], P("ldm", 0, 24, 1, 16 * gr, 16 * gr + 16)[1], P("ad", 3 * gr, 3 * gr + 3)[1])
+        ts(P("l6", 0, 12), PS(EX, 0, 12), sg(3), col(A6), A.mult, A.add)
+        keys("so6", "key6", 192, "r6", "sc6", P("l6", 0, 12))
+        owned(6, IND(P("key6", 0, 96), pl))
+        count(6, "cm6", "c6", "m6", 96, P("key6", 96, 192))
+        x1 = [P("x1", t, t + 1) for t in range(3)]
+        ts(P("x1", 0, 3), ends("c6", 96), sg(6), None, A.mult)
+        lay(8, x1, "tx7")
+        xmm(2, EX)
+        xmm(3, FIN, True, False)
+        act(heads("cm7", 192), ends("c6", 96), F_.Identity, bias=col(K7L), scale=col(SSC + 5))
+        act(P("fb", 768, 1152), PS(3, 0, 384))
+        act(P("bc", 0, 384), IND(P("ioc", 0, 384), P("lb7", 0, 24)))
+        act(P("fb", 1152, 1536), PS(1, 0, 384))
+        for b in range(4):
+            act(P("fh", 384 * b, 384 * b + 384), P("fb", 384 * b, 384 * b + 384), scale=0.5)
+        ts(pl, P("x1", 0, 3), 103.5, None, A.add)
+        ts(P("l7", 0, 24), PS(EX, 0, 24), col(A7), None, A.add)
+        keys("so7", "key7", 384, "r7", "sc7", P("l7", 0, 24))
+        owned(7, IND(P("key7", 0, 192), pl))
+        count(7, "cm7", "c7", "m7", 192, P("key7", 192, 384))
+        ts(P("x1", 0, 3), ends("c7", 192), sg(7), -7.5, A.mult, A.add)
+        lay(8, x1, "tx7")
+        xmm(4, FIN, False, True)
+        ts(P("plu", 0, 24, 1, 0, 96), P("ldm", 0, 24, 1, 0, 96), P("cc", O16, O16 + 1, 1, 0, 96), None, A.add)
+        ts(P("plu", 0, 24, 1, 96, 128), PS(FIN, 0, 24, 96, 128), P("cc", AF, AF + 1, 1, 96, 128), None, A.add)
+        tc(IND(P("w1", 0, 768), P("plu", 0, 24)), P("bc", 0, 384))
+        tr(P("t1", 0, 768), P("w1", 0, 768))
+        tt(P("ow", 0, 24), P("t1", 0, 768, 32), P("t1", 16, 768, 32), A.add)
+        ts(P("lz", 0, 24), P("ow", 0, 24), 192.0, None, A.add)
+        for b in range(4):
+            act(P("az", 192 * b, 192 * b + 192), IND(P("fb", 384 * b, 384 * b + 384), P("lz", 0, 12)), scale=0.5)
+        for b in range(4):
+            tt(P("zt", b, 768, 4), IND(P("fh", 384 * b, 384 * b + 384), P("lz", 12, 24)), P("az", 192 * b, 192 * b + 192), A.add)
+        zc, zs = P("zc%d" % r, 0, H), P("zs%d" % r, 0, H)
+        quant(zc, zs, P("zt", 0, 768))
+        need("g", "sv", cnt["sv"])
+        g.remote_dma(T["lc%d" % r][:, 0:H].bitcast(dt.uint8), zc[0].bitcast(dt.uint8), T.sem["ar%d" % r], T.sem.lsem, pid, rid, mask_c)
+        g.remote_dma(T["ls%d" % r][:, 0:H], zs[0], T.sem["ar%d" % r], T.sem.lsem, pid, rid, mask_s)
+        act(P("odf", 0, 384), IND(P("w1", 0, 768), P("stl", 0, 24)), F_.Identity, bias=192.0)
+        if last:
+            dma("y", "dout", T.od[:, :], T.odf[0:128:16, :], [], P("odf", 0, 384)[1])
+        else:
+            base_out()
+            act(P("odx", 0, 384), IND(P("w1", 0, 768), P("stl", 24, 48)), F_.Identity, bias=192.0)
+            base_out("odx", "dbx", "bxf")
+        if r == 0:
+            fill(P("w2", 0, 768), 0.0)
+        ts(P("h2", 0, 24), P("ow", 0, 24), 184.5, MAG, A.add, A.add)
+        ts(P("h2", 0, 24), P("h2", 0, 24), MAG - 192.0, col(O16), A.subtract, A.add)
+        tt(P("aj", 0, 24), P("h2", 0, 24), P("ow", 0, 24), A.add)
+        tc(P("lj", 0, 24), P("aj", 0, 24))
+        tc(IND(P("w2", 0, 768), P("lj", 0, 24)), P("km", 0, 384))
+        tr(P("t2", 0, 768), P("w2", 0, 768))
+        tt(P("iw", 0, 24), P("t2", 0, 768, 32), P("t2", 16, 768, 32), A.add)
+        tc(P("lr", 0, 24), P("iw", 0, 24))
+        fmm(3, BF3)
+        if r == 0:
+            quant(P("vc", 0, 128), P("vs", 0, 128), P("vt", 0, 512))
+        pb = lambda b: P("psb", 192 * b, 192 * b + 192)
+        for n, b in enumerate((3, 0, 1, 2)):
+            mm(PS(n, 0, H), P("wq", 128 * b, 128 * b + 128), P("wsc", 128 * b, 128 * b + 128), P("lc%d" % r, 0, H), P("ls%d" % r, 0, H), pre=[("ar%d" % r, 2 * half)])
+        act(pb(3), PS(0, 0, H), scale=0.03125)
+        ts(pb(0), PS(1, 0, H), 0.03125, None, A.mult)
+        act(pb(1), PS(2, 0, H), scale=0.03125)
+        act(pb(2), PS(3, 0, H), scale=0.03125)
+        act(P("g3", 0, 384), IND(pb(3), P("lr", 0, 24)))
+        for b in range(3):
+            tt(P("xt", b, 1536, 4), IND(pb(b), P("lr", 0, 24)), P("fb", 384 * b, 384 * b + 384), A.add)
+        tt(P("xt", 3, 1536, 4), P("g3", 0, 384), PS(BF3, 0, 384), A.add)
+    scores_in()
+    for h in range(2):
+        a, b = 192 * h, 192 * h + 192
+        q = P("xc", a, b)
+        dma("y", "dout", T.oc[:, 4 * a:4 * b], q[0].bitcast(dt.uint8), [], q[1])
+        mm(PS(h, 0, 192), P("vc", 0, 128), P("vs", 0, 128), q, P("xs", a, b))
+        if h == 0:
+            tc(P("yb", a, b), PS(h, 0, 192))
+        else:
+            act(P("yb", a, b), PS(h, 0, 192))
+        dma("y", "dout", T.y[:, a:b], T.yb[:, a:b], [], P("yb", a, b)[1])
+    for k in range(4):
+        dma("y", "dout", T.osc[4 * k:4 * k + 4, :], T.xs[32 * k:32 * k + 4, :], [], P("xs", 0, 384)[1])
+    g.wait_ge(T.sem.lsem, 2 * half * NR)
+    for s in list(cnt):
+        need("g", s, cnt[s])

@@ -7,11 +7,11 @@ W = [1, 3, 6, 12, 24, 48, 96, 192]
 SCRATCH = {"ps": ("psum", [128, 4096], "float32")}
 ALIAS = {}
 for _d, _s in (
-    ("float32", "cc:64 bof:3 bxf:3 bdf:3 gx:96 dx:48 bb:48 own:48 dd:3 c7:579 pg:18 hm:18 ad:18 ldm:24 xm:24 x1:3 ow:24 h2:24 aj:24 iw:24 odf:384 odx:384 psb:768 g3:384 yb:384 sgb:3072 mk:48 a24f:24"),
-    ("bfloat16", "ioc:384 km:384 on:128 m4:147 m6:291 m7:579 idt:384 ea:2048 eb:2560 ut:512 vt:512 xt:1536 fb:1536 fh:1536 cm:147 c4:147 cm6:291 c6:291 cm7:579 tx5:512 tx6:512 tx7:512 bc:384 "
+    ("float32", "cc:64 bof:3 bxf:3 bdf:3 gx:96 dx:48 bb:48 own:48 dd:3 pg:18 hm:18 ad:18 ldm:24 xm:24 x1:3 ow:24 h2:24 aj:24 iw:24 odf:384 odx:384 psb:768 g3:384 yb:384 sgb:3072 mk:48 a24f:24"),
+    ("bfloat16", "ioc:384 km:384 on:128 m4:147 m6:291 m7:579 idt:384 ea:2048 eb:2560 ut:512 vt:512 xt:1536 fb:1536 fh:1536 cm:147 c4:147 cm6:291 c6:291 cm7:579 c7:579 tx5:512 tx6:512 tx7:512 bc:384 "
                  "w1:768 t1:768 w2:768 t2:768 az:768 zt:768"),
     ("int32", "pi:1 pw:16 bi:8 uli:64 a24:24 pin:24"),
-    ("uint16", "ul:64 stl:48 lp0:24 lbox:6 lbp:3 lb5:3 lb6:12 lb7:24 pl:4 plo:4 l6:12 l7:24 plu:24 lz:24 lj:24 lr:24"),
+    ("uint16", "ul:64 stl:48 lp0:24 lbox:6 lbp:3 brow:384 lb5:3 lb6:12 lb7:24 pl:4 plo:4 l6:12 l7:24 plu:24 lz:24 lj:24 lr:24"),
     ("float8_e4m3fn_x4", "eac:512 ebc:640 uc:128 uqc:1024 vc:128 wq:512 xc:384 tc:128 zc0:192 zc1:192 zc2:192 lc0:192 lc1:192 lc2:192"),
     ("uint8", "eas:512 ebs:640 us:128 uqs:1024 vs:128 wsc:512 xs:384 tsc:128 zs0:192 zs1:192 zs2:192 ls0:192 ls1:192 ls2:192"),
 ):
@@ -24,7 +24,7 @@ for _b, _s in (("kc", "fi:48 posr:48 aa:48 r2:48 r3:48 r4:48 r5:48 r6:192 r7:384
         ALIAS[_w.split(":")[0]] = (_b, _o)
         _o += int(_w.split(":")[1])
     SCRATCH[_b] = ("sbuf", [128, _o], "float32")
-SEMAPHORES = ["sv", "ss", "st", "sg", "ar0", "ar1", "ar2", "lsem", "dp", "dxin", "du", "dv", "dwc", "dws", "db5", "db6", "db7", "dl", "dbo", "dbx", "dout"]
+SEMAPHORES = ["sv", "ss", "st", "sg", "ar0", "ar1", "ar2", "lsem", "dp", "dxin", "du", "dv", "dwc", "dws", "db5", "db6", "db7", "dbr", "dl", "dbo", "dbx", "dout"]
 
 
 def rank_program(g, core, T, topo):
@@ -67,8 +67,9 @@ def rank_program(g, core, T, topo):
                 if qs == own and (not hit(r, q) or not (wr or qw) or (e == "t" and wr)):
                     continue
                 todo[qs] = max(todo.get(qs, 0), qv)
-        for a_, b_ in list(todo.items()) + list(pre):
-            need(e, a_, cnt[a_] if a_ in dmh else b_)
+        for a_, b_ in sorted(todo.items(), key=lambda z: z[0] in dmh) + list(pre):
+            if known[e].get(a_, 0) < b_:
+                need(e, a_, cnt[a_] if a_ in dmh else b_)
         inc = 1 if sem is None else 16
         make().then_inc(T.sem[s], inc)
         cnt[s] = cnt.get(s, 0) + inc
@@ -166,10 +167,10 @@ def rank_program(g, core, T, topo):
     io(P("pi", 0, 1), [[0, 1]], 0, 1, False)
     io(P("uli", 0, 64), [[16, 8], [0, 8]], small=False)
     io(P("fi", 0, 48), [[0, 3], [1, 16]])
-    io(P("posr", 0, 48), [[1, 48]])
-    io(P("ioc", 0, 384), [[1, 384]], -192)
-    io(P("x8", 0, 8), [[1, 8]])
     io(P("pst", 0, 3), [[1, 3]], 0, 3)
+    io(P("ioc", 0, 384), [[1, 384]], -192)
+    io(P("posr", 0, 48), [[1, 48]])
+    io(P("x8", 0, 8), [[1, 8]])
     io(P("a24", 0, 24), [[32, 24]], small=False)
     ON, o6, o7 = P("on", 0, 128), P("idt", 128, 256), P("idt", 256, 384)
     fill(ON, 1.0)
@@ -181,6 +182,9 @@ def rank_program(g, core, T, topo):
     sel(o6, o6, [[64, 2], [0, 4], [4, 16]], A.is_ge, 3, -1)
     sel(o7, ON, [[0, 8], [-8, 16]], A.is_ge, 0, 1)
     sel(o7, o7, [[0, 8], [8, 16]], A.is_ge, 7, -1)
+    io(P("eb", 0, 2560), [[0, 2560]])
+    for n, w, c in (("m6", 291, 1), ("m7", 579, 1), ("w1", 768, 0), ("w2", 768, 0)):
+        io(P(n, 0, w), [[0, w]], c)
     io(P("km", 0, 384), [[0, 2], [1, 192]])
     for b in range(7):
         ts(P("bi", b, b + 1), P("pi", 0, 1), b, 1, A.logical_shift_right, A.bitwise_and)
@@ -227,7 +231,6 @@ def rank_program(g, core, T, topo):
     def xmm(k, bank, start=True, stop=True):
         mm(PS(bank, 0, 128), P("ebc", 128 * k, 128 * k + 128), P("ebs", 128 * k, 128 * k + 128), P("tc", 0, 128), P("tsc", 0, 128), start, stop)
 
-    scores_in()
     own = P("tmp", 0, 48)
     ts(own, P("fi", 0, 48), col(PM), None, A.is_equal)
     ts(P("aa", 0, 48), own, -1.0, 1.0, A.mult, A.add)
@@ -241,10 +244,11 @@ def rank_program(g, core, T, topo):
     ts(TA, col(PM), sg(1), None, A.add)
     ts(P("tmp", 48, 96), P("fi", 0, 48), TA, None, A.is_equal)
     ts(P("bm", 0, 48), P("tmp", 48, 96), 0.0, col(S29), A.is_equal, A.mult)
-    fill(P("r2", 0, 768), 0.0)
     fill(P("m4", 0, 147), 1.0)
     fill(P("m4", 0, 147, 49), 0.0)
+    scores_in()
     mode["defer"] = True
+    fill(P("r2", 0, 192), 0.0)
     for k in (2, 3, 4):
         ts(TA, col(T0 + k - 2), sg(k), float(W[k]), A.add, A.mult)
         ts(TB, TA, float(W[k]), None, A.add)
@@ -254,18 +258,12 @@ def rank_program(g, core, T, topo):
         tt(P("tmp", 48, 96), P("tmp", 48, 96), P("tmp", 96, 144), A.subtract)
         ts(P("bm", 48 * k - 48, 48 * k), P("tmp", 48, 96), 0.0, col(S29 + k - 1), A.is_equal, A.mult)
     quant(P("eac", 0, 512), P("eas", 0, 512), P("ea", 0, 2048))
+    fill(P("r6", 0, 576), 0.0)
     for n in (5, 6, 7):
         fill(P("r%d" % n, 0, 48 if n < 6 else 2 * W[n], W[n]), -BIG)
-    fill(P("eb", 0, 2560), 0.0)
-    for k, (src, a, b, wt) in enumerate(((0, 0, 128, 1.0), (128, 0, 128, 1.0), (256, 0, 128, 1.0), (256, 96, 112, 2.0), (256, 112, 128, 2.0))):
-        for d in range(2):
-            ts(P("eb", 512 * k + 4 * a + d, 512 * k + 4 * b, 4), P("idt", src + a, src + b), wt if d == 0 else 1.0, None, A.mult)
     for n in ("tx5", "tx6", "tx7"):
         fill(P(n, 0, 512), 0.0)
-    quant(P("ebc", 0, 512), P("ebs", 0, 512), P("eb", 0, 2048))
-    quant(P("ebc", 512, 640), P("ebs", 512, 640), P("eb", 2048, 2560))
     for n, w in (("m6", 96), ("m7", 192)):
-        fill(P(n, 0, 3 * w + 3), 1.0)
         fill(P(n, 0, 3 * w + 3, w + 1), 0.0)
     ts(col(Q96), col(T0 + 3), 96.0, None, A.mult)
     ts(col(O16), bit(4), 16.0, None, A.mult)
@@ -278,6 +276,11 @@ def rank_program(g, core, T, topo):
     ts(col(A6), TA, TB, None, A.add)
     ts(P("mx4", 0, 4), P("x8", 0, 4), col(PM3), None, A.is_equal)
     ts(P("mx8", 0, 8), P("x8", 0, 8), col(PM7), None, A.is_equal)
+    for k, (src, a, b, wt) in enumerate(((0, 0, 128, 1.0), (128, 0, 128, 1.0), (256, 0, 128, 1.0), (256, 96, 112, 2.0), (256, 112, 128, 2.0))):
+        for d in range(2):
+            ts(P("eb", 512 * k + 4 * a + d, 512 * k + 4 * b, 4), P("idt", src + a, src + b), wt if d == 0 else 1.0, None, A.mult)
+    quant(P("ebc", 0, 512), P("ebs", 0, 512), P("eb", 0, 2048))
+    quant(P("ebc", 512, 640), P("ebs", 512, 640), P("eb", 2048, 2560))
     ts(TA, sg(7), 103.5, None, A.mult)
     ts(TB, bit(6), 192.0, -192.0, A.mult, A.add)
     ts(col(K7L), TA, TB, None, A.add)
@@ -286,7 +289,6 @@ def rank_program(g, core, T, topo):
     ts(TA, bit(3), 384.0, 199.5, A.mult, A.add)
     ts(TB, bit(3), -384.0, 208.0, A.mult, A.add)
     ts(col(AF), TB, bit(4), TA, A.mult, A.add)
-    fill(P("w1", 0, 768), 0.0)
     tc(P("a24f", 0, 24), P("a24", 0, 24))
     tt(col(PMX), col(PM31), sg(1), A.add)
     ts(P("stl", 0, 24), P("a24f", 0, 24), col(PM31), None, A.add)
@@ -352,16 +354,20 @@ def rank_program(g, core, T, topo):
         for t in range(3):
             ts(P("lbp", t, t + 1), P("dd", t, t + 1), P("bdf", t, t + 1), P("bof", t, t + 1), A.mult, A.add)
         lp = P("lbp", 0, 3)
-        for name, n, src in (("lb5", 3, lambda q: (16 * (q + 1 - 2 * (q % 2)), 16)), ("lb6", 12, lambda q: (64 * (q // 4), 64)), ("lb7", 24, lambda q: (0, 128))):
+        dma("y", "dbr", T.brow[0:1, 0:384], T.lbp[:, :], P("brow", 0, 384, 1, 0, 1)[1], lp[1])
+        for name, n, src in (("lb5", 3, lambda q: (16 * (q + 1 - 2 * (q % 2)), 16)), ("lb6", 12, lambda q: (64 * (q // 4), 64))):
             for q in range(8):
                 a, m = src(q)
                 dma("y", "db" + name[2], T[name][16 * q:16 * q + 16, 0:n], T.lbp[a:a + m, 0:3], P(name, 0, n, 1, 16 * q, 16 * q + 16)[1], P("lbp", 0, 3, 1, a, a + m)[1])
-        for k in (1, 2):
-            act(SGR(k), PS(k + 1, 0, 384))
-            act(P("sc%d" % k, 0, 48), IND(SGR(k), lp))
-            if k == 1:
-                act(heads("cm", 48), P("psl", 0, 3))
-            smm(4 + k, k + 1)
+        for q in range(8):
+            dma("y", "db7", T.lb7[16 * q:16 * q + 16, 0:24], T.brow[0:1, 0:384], P("lb7", 0, 24, 1, 16 * q, 16 * q + 16)[1], P("brow", 0, 384, 1, 0, 1)[1])
+        act(SGR(1), PS(2, 0, 384))
+        act(heads("cm", 48), P("psl", 0, 3))
+        smm(5, 2)
+        act(SGR(2), PS(3, 0, 384))
+        act(P("sc2", 0, 48), IND(SGR(2), lp))
+        smm(6, 3)
+        tc(P("sc1", 0, 48), IND(SGR(1), lp))
         tt(P("sc1", 16, 32), P("sc1", 16, 32), P("sc1", 0, 16), A.max)
         tt(P("sc1", 32, 48), P("sc1", 32, 48), P("sc1", 16, 32), A.max)
         owned(1, P("sc1", 0, 48))
@@ -381,7 +387,7 @@ def rank_program(g, core, T, topo):
                 fmm(0, 1)
             else:
                 act(P("sc5o", 0, 48), IND(SGR(5), P("lb5", 0, 3)))
-        flush(23)
+        flush(12)
         ts(P("tx5", 0, 12, 4), ends("c4", 48), MAG, MAG, A.add, A.subtract)
         tt(P("tx5", 1, 12, 4), ends("c4", 48), P("tx5", 0, 12, 4), A.subtract)
         quant(P("tc", 0, 128), P("tsc", 0, 128), P("tx5", 0, 512))
@@ -460,8 +466,6 @@ def rank_program(g, core, T, topo):
             base_out()
             act(P("odx", 0, 384), IND(P("w1", 0, 768), P("stl", 24, 48)), F_.Identity, bias=192.0)
             base_out("odx", "dbx", "bxf")
-        if r == 0:
-            fill(P("w2", 0, 768), 0.0)
         ts(P("h2", 0, 24), P("ow", 0, 24), 184.5, MAG, A.add, A.add)
         ts(P("h2", 0, 24), P("h2", 0, 24), MAG - 192.0, col(O16), A.subtract, A.add)
         tt(P("aj", 0, 24), P("h2", 0, 24), P("ow", 0, 24), A.add)

@@ -7,7 +7,7 @@ W = [1, 3, 6, 12, 24, 48, 96, 192]
 SCRATCH = {"ps": ("psum", [128, 4096], "float32")}
 ALIAS = {}
 for _d, _s in (
-    ("float32", "cc:64 bof:3 bxf:3 bdf:3 gx:96 dx:48 bb:48 own:48 dd:3 pg:18 hm:18 ad:18 ldm:24 xm:24 x1:3 ow:24 h2:24 aj:24 iw:24 odf:384 odx:384 psb:768 g3:384 yb:384 sgb:3072 mk:48 a24f:24"),
+    ("float32", "cc:64 bof:3 bxf:3 bdf:3 b0:96 b1:48 bb:48 own:96 dd:3 os:3 pg:18 hm:18 ad:18 ldm:24 xm:24 x1:3 ow:24 h2:24 aj:24 iw:24 odf:384 odx:384 psb:768 g3:384 yb:384 sgb:3072 mk:48 a24f:24"),
     ("bfloat16", "ioc:384 km:384 on:128 m4:147 m6:291 m7:579 idt:384 ea:2048 eb:2560 ut:512 vt:512 xt:1536 fb:1536 fh:1536 cm:147 c4:147 cm6:291 c6:291 cm7:579 c7:579 tx5:512 tx6:512 tx7:512 bc:384 "
                  "w1:768 t1:768 w2:768 t2:768 az:768 zt:768"),
     ("int32", "pi:1 pw:16 bi:8 uli:64 a24:24 pin:24"),
@@ -17,8 +17,8 @@ for _d, _s in (
 ):
     for _w in _s.split():
         SCRATCH[_w.split(":")[0]] = ("sbuf", [128, int(_w.split(":")[1])], _d)
-for _b, _s in (("kc", "fi:48 posr:48 aa:48 r2:48 r3:48 r4:48 r5:48 r6:192 r7:384 x8:16 mx4:16 mx8:16 pst:16 psl:16 tmp:144 om:384 bm:192"), ("sc", "sc1:48 sc2:48 sc3:48 sc4:48 sc5:48 sc5o:48 sc6:192 sc7:384"),
-               ("so", "so:48 so5:48 so6:192 so7:384"), ("key", "key:48 key5:48 key6:192 key7:384")):
+for _b, _s in (("kc", "fi:48 posr:48 aa:96 r2:48 r3:48 r4:48 r5:48 r6:192 r7:384 x8:16 mx4:16 mx8:16 mx8s:16 pst:16 psl:16 tmp:144 om:384 om0:96 ng:48 bm:192"),
+               ("sc", "sc1:48 sc2:48 sc3:48 sc4:48 sc5:48 sc5o:48 sc6:192 sc7:384"), ("so", "so:48 so5:48 so6:192 so7:384"), ("key", "key:48 key5:48 key6:192 key7:384")):
     _o = 0
     for _w in _s.split():
         ALIAS[_w.split(":")[0]] = (_b, _o)
@@ -179,27 +179,24 @@ def rank_program(g, core, T, topo):
         sel(P("ea", 512 * b + b, 512 * b + 512, 4), ON, [[-1, 128]], A.is_equal, 0, 1)
     sel(P("idt", 0, 128), ON, [[-32, 4], [16, 2], [-1, 16]], A.is_equal, -16, 1)
     sel(o6, ON, [[-64, 2], [0, 4], [-4, 16]], A.is_ge, 0, 1)
-    sel(o6, o6, [[64, 2], [0, 4], [4, 16]], A.is_ge, 3, -1)
     sel(o7, ON, [[0, 8], [-8, 16]], A.is_ge, 0, 1)
+    sel(o6, o6, [[64, 2], [0, 4], [4, 16]], A.is_ge, 3, -1)
     sel(o7, o7, [[0, 8], [8, 16]], A.is_ge, 7, -1)
-    io(P("eb", 0, 2560), [[0, 2560]])
-    for n, w, c in (("m6", 291, 1), ("m7", 579, 1), ("w1", 768, 0), ("w2", 768, 0)):
+    for n, w, c in (("eb", 2560, 0), ("tx5", 512, 0), ("r6", 576, 0), ("tx6", 512, 0), ("m6", 291, 1), ("tx7", 512, 0), ("m7", 579, 1), ("w1", 768, 0), ("w2", 768, 0)):
         io(P(n, 0, w), [[0, w]], c)
     io(P("km", 0, 384), [[0, 2], [1, 192]])
     for b in range(7):
         ts(P("bi", b, b + 1), P("pi", 0, 1), b, 1, A.logical_shift_right, A.bitwise_and)
     for k, m in ((0, 15), (1, 3), (2, 7), (3, 31)):
         ts(P("pw", k, k + 1), P("pi", 0, 1), m, None, A.bitwise_and)
+    ts(P("pw", 8, 9), P("pi", 0, 1), 4, None, A.logical_shift_right)
     for k in (1, 2, 3):
         ts(P("pw", 4 + k, 5 + k), P("pw", 0, 1), k, None, A.logical_shift_right)
-    ts(P("pw", 8, 9), P("pi", 0, 1), 4, None, A.logical_shift_right)
     tc(P("cc", BFC, BFC + 7), P("bi", 0, 7))
     tc(P("cc", PM, PM + 4), P("pw", 0, 4))
-    tc(P("cc", T0, T0 + 4), P("pw", 5, 9))
     tc(P("ul", 0, 64), P("uli", 0, 64))
+    tc(P("cc", T0, T0 + 4), P("pw", 5, 9))
     ts(P("cc", SGC, SGC + 7), P("cc", BFC, BFC + 7), -2.0, 1.0, A.mult, A.add)
-    ts(P("cc", S29, S29 + 4), P("cc", SGC, SGC + 4), BIG, None, A.mult)
-    tt(P("cc", SSC, SSC + 6), P("cc", SGC, SGC + 6), P("cc", SGC + 1, SGC + 7), A.mult)
 
     def base_out(e="odf", sem="dbo", to="bof", p=112):
         dma("y", sem, T[to][:, :], T[e][p:p + 1, :], P(to, 0, 3)[1], P(e, 0, 384)[1])
@@ -207,14 +204,16 @@ def rank_program(g, core, T, topo):
     tc(P("lp0", 0, 24), P("pin", 0, 24))
     act(P("odf", 0, 384), IND(P("ioc", 0, 384), P("lp0", 0, 24)), F_.Identity, bias=192.0)
     base_out()
+    ts(P("cc", S29, S29 + 4), P("cc", SGC, SGC + 4), BIG, None, A.mult)
+    tt(P("cc", SSC, SSC + 6), P("cc", SGC, SGC + 6), P("cc", SGC + 1, SGC + 7), A.mult)
+    uw, uo, ul = P("uc", 0, 128), P("uqc", 0, 1024), P("ul", 0, 64)
+    quant(uw, P("us", 0, 128), P("ut", 0, 512))
     tc(P("odx", 0, 384, 2), P("odf", 1, 384, 2))
     tc(P("odx", 1, 384, 2), P("odf", 0, 384, 2))
     base_out("odx", "dbx", "bxf")
     dma("y", "dwc", T.wq[:, :].bitcast(dt.uint8), T.wc[:, :], P("wq", 0, 512)[1], [])
     dma("y", "dws", T.wsc[:, :], T.ws[:, :], P("wsc", 0, 512)[1], [])
     dma("y", "dv", T.vt[:, :], T.v[:, :], P("vt", 0, 512)[1], [])
-    uw, uo, ul = P("uc", 0, 128), P("uqc", 0, 1024), P("ul", 0, 64)
-    quant(uw, P("us", 0, 128), P("ut", 0, 512))
     act(P("uqs", 0, 1024), IND(P("us", 0, 128), ul))
     op("v", lambda: g.vector.tensor_copy(uo[0].bitcast(dt.uint32), uw[0].bitcast(dt.uint32).indirect(ul[0])), uo[1], uw[1] + ul[1])
 
@@ -233,22 +232,24 @@ def rank_program(g, core, T, topo):
 
     own = P("tmp", 0, 48)
     ts(own, P("fi", 0, 48), col(PM), None, A.is_equal)
-    ts(P("aa", 0, 48), own, -1.0, 1.0, A.mult, A.add)
-    for t in range(3):
-        ts(P("om", 16 * t, 16 * t + 16), P("tmp", 16 * t, 16 * t + 16), sg(1), 1.0 if t != 1 else -1.0, A.mult, A.mult)
-    for k in range(1, 8):
-        ts(P("om", 48 * k, 48 * k + 48), own, sg(k), None, A.mult)
     ts(TB, col(T0 + 3), -48.0, None, A.mult)
-    ts(P("pg", 0, 3), P("pst", 0, 3), TB, None, A.add)
-    ts(P("psl", 0, 3), P("pg", 0, 3), sg(1), None, A.mult)
     ts(TA, col(PM), sg(1), None, A.add)
-    ts(P("tmp", 48, 96), P("fi", 0, 48), TA, None, A.is_equal)
-    ts(P("bm", 0, 48), P("tmp", 48, 96), 0.0, col(S29), A.is_equal, A.mult)
     fill(P("m4", 0, 147), 1.0)
+    for h in (0, 48):
+        ts(P("aa", h, h + 48), own, -1.0, 1.0, A.mult, A.add)
+        for t in range(3):
+            ts(P("om0", h + 16 * t, h + 16 * t + 16), P("tmp", 16 * t, 16 * t + 16), sg(1), 1.0 if t != 1 else -1.0, A.mult, A.mult)
+    ts(P("pg", 0, 3), P("pst", 0, 3), TB, None, A.add)
+    ts(P("tmp", 48, 96), P("fi", 0, 48), TA, None, A.is_equal)
+    ts(P("ng", 0, 48), P("aa", 0, 48), -BIG, None, A.mult)
     fill(P("m4", 0, 147, 49), 0.0)
+    ts(P("psl", 0, 3), P("pg", 0, 3), sg(1), None, A.mult)
+    ts(P("bm", 0, 48), P("tmp", 48, 96), 0.0, col(S29), A.is_equal, A.mult)
     scores_in()
     mode["defer"] = True
     fill(P("r2", 0, 192), 0.0)
+    for k in (2, 3, 4, 5, 6, 7):
+        ts(P("om", 48 * k, 48 * k + 48), own, sg(k), None, A.mult)
     for k in (2, 3, 4):
         ts(TA, col(T0 + k - 2), sg(k), float(W[k]), A.add, A.mult)
         ts(TB, TA, float(W[k]), None, A.add)
@@ -258,13 +259,8 @@ def rank_program(g, core, T, topo):
         tt(P("tmp", 48, 96), P("tmp", 48, 96), P("tmp", 96, 144), A.subtract)
         ts(P("bm", 48 * k - 48, 48 * k), P("tmp", 48, 96), 0.0, col(S29 + k - 1), A.is_equal, A.mult)
     quant(P("eac", 0, 512), P("eas", 0, 512), P("ea", 0, 2048))
-    fill(P("r6", 0, 576), 0.0)
     for n in (5, 6, 7):
         fill(P("r%d" % n, 0, 48 if n < 6 else 2 * W[n], W[n]), -BIG)
-    for n in ("tx5", "tx6", "tx7"):
-        fill(P(n, 0, 512), 0.0)
-    for n, w in (("m6", 96), ("m7", 192)):
-        fill(P(n, 0, 3 * w + 3, w + 1), 0.0)
     ts(col(Q96), col(T0 + 3), 96.0, None, A.mult)
     ts(col(O16), bit(4), 16.0, None, A.mult)
     ts(TA, bit(4), 48.0, sg(6), A.mult, A.mult)
@@ -281,6 +277,9 @@ def rank_program(g, core, T, topo):
             ts(P("eb", 512 * k + 4 * a + d, 512 * k + 4 * b, 4), P("idt", src + a, src + b), wt if d == 0 else 1.0, None, A.mult)
     quant(P("ebc", 0, 512), P("ebs", 0, 512), P("eb", 0, 2048))
     quant(P("ebc", 512, 640), P("ebs", 512, 640), P("eb", 2048, 2560))
+    for n, w in (("m6", 96), ("m7", 192)):
+        fill(P(n, 0, 3 * w + 3, w + 1), 0.0)
+    ts(P("mx8s", 0, 8), P("mx8", 0, 8), sg(6), None, A.mult)
     ts(TA, sg(7), 103.5, None, A.mult)
     ts(TB, bit(6), 192.0, -192.0, A.mult, A.add)
     ts(col(K7L), TA, TB, None, A.add)
@@ -313,20 +312,27 @@ def rank_program(g, core, T, topo):
         tc(IND(P(so, 0, n), lst), P(sc, 0, n))
         scan(P(key, 0, n), P(res, 0, n), P(so, 0, n), -BIG, A.add, A.max)
 
+    def halves(so, key, res, w):
+        for h in (0, w):
+            scan(P(key, h, h + w), P(res, h, h + w), P(so, h, h + w), -BIG, A.add, A.max)
+
     def owned(k, src):
         tt(P("bb", 0, 48), src, P("om", 48 * k, 48 * k + 48), A.mult)
-        if k in (1, 2, 3, 4):
-            tt(P("mk", 0, 48), P("sc1" if k == 1 else "key", 0, 48), P("bm", 48 * k - 48, 48 * k), A.add)
+        if k in (2, 3, 4):
+            tt(P("mk", 0, 48), P("key", 0, 48), P("bm", 48 * k - 48, 48 * k), A.add)
         scan(P("own", 0, 48), P("aa", 0, 48), P("bb", 0, 48), 0.0, A.mult, A.add)
 
-    def count(k, cmn, cn, mn, w, other):
+    def count(k, cmn, cn, mn, w, other, mine=("own", 15, 16), parts=1):
         for t in range(3):
-            ts(P(cmn, (w + 1) * t + 1, (w + 1) * t + w + 1), other, sg(k), P("own", 16 * t + 15, 16 * t + 16), A.mult, A.is_lt)
-        scan(P(cn, 0, 3 * w + 3), P(mn, 0, 3 * w + 3), P(cmn, 0, 3 * w + 3), 0.0, A.mult, A.add)
+            o = mine[1] + mine[2] * t
+            ts(P(cmn, (w + 1) * t + 1, (w + 1) * t + w + 1), other, sg(k), P(mine[0], o, o + 1), A.mult, A.is_lt)
+        n = (3 * w + 3) // parts
+        for a in range(0, 3 * w + 3, n):
+            scan(P(cn, a, a + n), P(mn, a, a + n), P(cmn, a, a + n), 0.0, A.mult, A.add)
 
-    def lay(n, xs, tile):
+    def lay(n, xs, tile, mask):
         for t in range(3):
-            ts(P("xm", t, 3 * n, 3), P("mx%d" % n, 0, n), xs[t], None, A.mult)
+            ts(P("xm", t, 3 * n, 3), P(mask, 0, n), xs[t], None, A.mult)
         ts(P(tile, 0, 12 * n, 4), P("xm", 0, 3 * n), MAG, MAG, A.add, A.subtract)
         tt(P(tile, 1, 12 * n, 4), P("xm", 0, 3 * n), P(tile, 0, 12 * n, 4), A.subtract)
         quant(P("tc", 0, 128), P("tsc", 0, 128), P(tile, 0, 512))
@@ -343,14 +349,13 @@ def rank_program(g, core, T, topo):
         tc(P("lbox", 0, 3), P("bof", 0, 3))
         tc(P("lbox", 3, 6), P("bxf", 0, 3))
         tt(P("bdf", 0, 3), P("bxf", 0, 3), P("bof", 0, 3), A.subtract)
-        tc(P("sgb", 0, 192), PS(0, 0, 192))
-        act(P("sgb", 192, 384), PS(1, 0, 192))
+        act(P("sgb", 0, 192), PS(0, 0, 192))
+        tc(P("sgb", 192, 384), PS(1, 0, 192))
         smm(3, 0)
         smm(4, 1)
-        tc(P("gx", 0, 96), IND(SGR(0), P("lbox", 0, 6)))
-        tt(P("dx", 0, 48), P("gx", 0, 48), P("gx", 48, 96), A.subtract)
-        owned(0, P("dx", 0, 48))
-        ts(P("dd", 0, 3), P("own", 15, 48, 16), 0.0, None, A.is_gt)
+        tt(P("b0", 0, 96), IND(SGR(0), P("lbox", 0, 6)), P("om0", 0, 96), A.mult)
+        scan(P("own", 0, 96), P("aa", 0, 96), P("b0", 0, 96), 0.0, A.mult, A.add)
+        tt(P("dd", 0, 3), P("own", 15, 48, 16), P("own", 63, 96, 16), A.is_gt)
         for t in range(3):
             ts(P("lbp", t, t + 1), P("dd", t, t + 1), P("bdf", t, t + 1), P("bof", t, t + 1), A.mult, A.add)
         lp = P("lbp", 0, 3)
@@ -367,11 +372,14 @@ def rank_program(g, core, T, topo):
         act(SGR(2), PS(3, 0, 384))
         act(P("sc2", 0, 48), IND(SGR(2), lp))
         smm(6, 3)
-        tc(P("sc1", 0, 48), IND(SGR(1), lp))
+        s1, b1 = P("sc1", 0, 48), P("b1", 0, 48)
+        tt(s1, IND(SGR(1), lp), P("bm", 0, 48), A.add)
+        tt(b1, IND(SGR(1), lp), P("ng", 0, 48), A.add)
         tt(P("sc1", 16, 32), P("sc1", 16, 32), P("sc1", 0, 16), A.max)
+        scan(P("own", 0, 48), b1, b1, -BIG, A.max, A.max)
         tt(P("sc1", 32, 48), P("sc1", 32, 48), P("sc1", 16, 32), A.max)
-        owned(1, P("sc1", 0, 48))
-        count(1, "cm", "c4", "m4", 48, P("mk", 0, 48))
+        ts(P("os", 0, 3), P("own", 15, 48, 16), sg(1), None, A.mult)
+        count(1, "cm", "c4", "m4", 48, s1, ("os", 0, 1))
         for k in (2, 3, 4):
             ts(pl, ends("c4", 48), sg(k - 1), None, A.mult)
             act(heads("cm", 48), ends("c4", 48), scale=col(SSC + k - 2))
@@ -387,7 +395,7 @@ def rank_program(g, core, T, topo):
                 fmm(0, 1)
             else:
                 act(P("sc5o", 0, 48), IND(SGR(5), P("lb5", 0, 3)))
-        flush(12)
+        flush(15)
         ts(P("tx5", 0, 12, 4), ends("c4", 48), MAG, MAG, A.add, A.subtract)
         tt(P("tx5", 1, 12, 4), ends("c4", 48), P("tx5", 0, 12, 4), A.subtract)
         quant(P("tc", 0, 128), P("tsc", 0, 128), P("tx5", 0, 512))
@@ -401,12 +409,14 @@ def rank_program(g, core, T, topo):
         act(P("fb", 0, 384), PS(1, 0, 384))
         ts(pl, ends("c4", 48), sg(4), None, A.mult)
         keys("so", "key", 48, "r5", "sc5", pl)
-        owned(5, IND(P("key", 0, 48), pl))
         ts(plo, PS(EX, 0, 3), sg(4), None, A.mult)
-        keys("so5", "key5", 48, "r5", "sc5o", plo)
+        tt(P("bb", 0, 48), IND(P("key", 0, 48), pl), P("om", 240, 288), A.mult)
+        tc(IND(P("so5", 0, 48), plo), P("sc5o", 0, 48))
+        scan(P("own", 0, 48), P("aa", 0, 48), P("bb", 0, 48), 0.0, A.mult, A.add)
+        scan(P("key5", 0, 48), P("r5", 0, 48), P("so5", 0, 48), -BIG, A.add, A.max)
         count(5, "cm", "c4", "m4", 48, P("key5", 0, 48))
         flush(0)
-        lay(4, [P("c4", 49 * t + 48, 49 * t + 49) for t in range(3)], "tx6")
+        lay(4, [P("c4", 49 * t + 48, 49 * t + 49) for t in range(3)], "tx6", "mx4")
         xmm(1, EX)
         fmm(3, 1)
         act(heads("cm6", 96), ends("c4", 48), F_.Identity, bias=col(K6L), scale=col(SSC + 4))
@@ -416,18 +426,19 @@ def rank_program(g, core, T, topo):
         act(P("fb", 384, 768), PS(2, 0, 384))
         ts(pl, ends("c4", 48), sg(5), col(K5O), A.mult, A.add)
         a = 3 if r else 0
-        ts(P("hm", a, 18), P("pg", a, 18), -7.5, MAG, A.add, A.add)
-        ts(P("hm", a, 18), P("hm", a, 18), MAG, col(Q96), A.subtract, A.add)
-        tt(P("ad", a, 18), P("hm", a, 18), P("pg", a, 18), A.add)
+        hm, pg, ad = P("hm", a, 18), P("pg", a, 18), P("ad", a, 18)
+        ts(hm, pg, -7.5, MAG, A.add, A.add)
+        ts(P("l6", 0, 12), PS(EX, 0, 12), sg(3), col(A6), A.mult, A.add)
+        tc(IND(P("so6", 0, 192), P("l6", 0, 12)), P("sc6", 0, 192))
+        ts(hm, hm, MAG, col(Q96), A.subtract, A.add)
+        halves("so6", "key6", "r6", 96)
+        tt(P("bb", 0, 48), IND(P("key6", 0, 96), pl), P("om", 288, 336), A.mult)
+        tt(ad, hm, pg, A.add)
         for gr in range(a // 3, 6):
             dma("y", "dl", T.ldm[16 * gr:16 * gr + 16, 0:24], T.ad[:, 3 * gr:3 * gr + 3], P("ldm", 0, 24, 1, 16 * gr, 16 * gr + 16)[1], P("ad", 3 * gr, 3 * gr + 3)[1])
-        ts(P("l6", 0, 12), PS(EX, 0, 12), sg(3), col(A6), A.mult, A.add)
-        keys("so6", "key6", 192, "r6", "sc6", P("l6", 0, 12))
-        owned(6, IND(P("key6", 0, 96), pl))
-        count(6, "cm6", "c6", "m6", 96, P("key6", 96, 192))
-        x1 = [P("x1", t, t + 1) for t in range(3)]
-        ts(P("x1", 0, 3), ends("c6", 96), sg(6), None, A.mult)
-        lay(8, x1, "tx7")
+        scan(P("own", 0, 48), P("aa", 0, 48), P("bb", 0, 48), 0.0, A.mult, A.add)
+        count(6, "cm6", "c6", "m6", 96, P("key6", 96, 192), parts=3)
+        lay(8, [P("c6", 97 * t + 96, 97 * t + 97) for t in range(3)], "tx7", "mx8s")
         xmm(2, EX)
         xmm(3, FIN, True, False)
         act(heads("cm7", 192), ends("c6", 96), F_.Identity, bias=col(K7L), scale=col(SSC + 5))
@@ -436,13 +447,16 @@ def rank_program(g, core, T, topo):
         act(P("fb", 1152, 1536), PS(1, 0, 384))
         for b in range(4):
             act(P("fh", 384 * b, 384 * b + 384), P("fb", 384 * b, 384 * b + 384), scale=0.5)
-        ts(pl, P("x1", 0, 3), 103.5, None, A.add)
+        ts(pl, ends("c6", 96), sg(6), 103.5, A.mult, A.add)
         ts(P("l7", 0, 24), PS(EX, 0, 24), col(A7), None, A.add)
-        keys("so7", "key7", 384, "r7", "sc7", P("l7", 0, 24))
+        tc(IND(P("so7", 0, 384), P("l7", 0, 24)), P("sc7", 0, 384))
+        halves("so7", "key7", "r7", 192)
         owned(7, IND(P("key7", 0, 192), pl))
-        count(7, "cm7", "c7", "m7", 192, P("key7", 192, 384))
-        ts(P("x1", 0, 3), ends("c7", 192), sg(7), -7.5, A.mult, A.add)
-        lay(8, x1, "tx7")
+        count(7, "cm7", "c7", "m7", 192, P("key7", 192, 384), parts=3)
+        x1 = [P("x1", t, t + 1) for t in range(3)]
+        for t in range(3):
+            ts(x1[t], P("c7", 193 * t + 192, 193 * t + 193), sg(7), -7.5, A.mult, A.add)
+        lay(8, x1, "tx7", "mx8")
         xmm(4, FIN, False, True)
         ts(P("plu", 0, 24, 1, 0, 96), P("ldm", 0, 24, 1, 0, 96), P("cc", O16, O16 + 1, 1, 0, 96), None, A.add)
         ts(P("plu", 0, 24, 1, 96, 128), PS(FIN, 0, 24, 96, 128), P("cc", AF, AF + 1, 1, 96, 128), None, A.add)
@@ -450,7 +464,8 @@ def rank_program(g, core, T, topo):
         tr(P("t1", 0, 768), P("w1", 0, 768))
         tt(P("ow", 0, 24), P("t1", 0, 768, 32), P("t1", 16, 768, 32), A.add)
         ts(P("lz", 0, 24), P("ow", 0, 24), 192.0, None, A.add)
-        for b in range(4):
+        tc(P("az", 0, 192), IND(P("fh", 0, 384), P("lz", 0, 12)))
+        for b in range(1, 4):
             act(P("az", 192 * b, 192 * b + 192), IND(P("fb", 384 * b, 384 * b + 384), P("lz", 0, 12)), scale=0.5)
         for b in range(4):
             tt(P("zt", b, 768, 4), IND(P("fh", 384 * b, 384 * b + 384), P("lz", 12, 24)), P("az", 192 * b, 192 * b + 192), A.add)
@@ -478,12 +493,11 @@ def rank_program(g, core, T, topo):
         if r == 0:
             quant(P("vc", 0, 128), P("vs", 0, 128), P("vt", 0, 512))
         pb = lambda b: P("psb", 192 * b, 192 * b + 192)
-        for n, b in enumerate((3, 0, 1, 2)):
-            mm(PS(n, 0, H), P("wq", 128 * b, 128 * b + 128), P("wsc", 128 * b, 128 * b + 128), P("lc%d" % r, 0, H), P("ls%d" % r, 0, H), pre=[("ar%d" % r, 2 * half)])
-        act(pb(3), PS(0, 0, H), scale=0.03125)
-        ts(pb(0), PS(1, 0, H), 0.03125, None, A.mult)
-        act(pb(1), PS(2, 0, H), scale=0.03125)
-        act(pb(2), PS(3, 0, H), scale=0.03125)
+        for b in range(4):
+            mm(PS(b, 0, H), P("wq", 128 * b, 128 * b + 128), P("wsc", 128 * b, 128 * b + 128), P("lc%d" % r, 0, H), P("ls%d" % r, 0, H), pre=[("ar%d" % r, 2 * half)])
+        ts(pb(0), PS(0, 0, H), 0.03125, None, A.mult)
+        for b in range(1, 4):
+            act(pb(b), PS(b, 0, H), scale=0.03125)
         act(P("g3", 0, 384), IND(pb(3), P("lr", 0, 24)))
         for b in range(3):
             tt(P("xt", b, 1536, 4), IND(pb(b), P("lr", 0, 24)), P("fb", 384 * b, 384 * b + 384), A.add)

from concourse.mybir import dt, AluOpType as A, ActivationFunctionType as F_

NR, H = 3, 192
BIG = 1e29
MAG = 201326592.0
W = [1, 3, 6, 12, 24, 48, 96, 192]
SCRATCH = {"ps": ("psum", [128, 4096], "float32")}
ALIAS = {}
for _d, _s in (
    ("float32", "cc:64 bof:3 bxf:3 bdf:3 b0:96 b1:48 bb:48 own:96 dd:3 os:3 pg:18 hm:18 ad:18 ldm:24 xm:24 x1:3 ow:24 h2:24 aj:24 iw:24 odf:384 odx:384 psb:768 g3:384 yb:384 sgb:3072 mk:48 a24f:24"),
    ("bfloat16", "ioc:384 km:384 on:128 m4:147 m6:291 m7:579 idt:384 ea:2048 eb:2560 ut:512 vt:512 xt:1536 fb:1536 fh:1536 cm:147 c4:147 cm6:291 c6:291 cm7:579 c7:579 tx5:512 tx6:512 tx7:512 bc:384 "
                 "w1:768 t1:768 w2:768 t2:768 az:768 zt:768"),
    ("int32", "pi:1 pw:16 bi:8 uli:64 a24:24 pin:24"),
    ("uint16", "ul:64 stl:48 lp0:24 lbox:6 lbp:3 brow:384 lb5:3 lb6:12 lb7:24 pl:4 plo:4 l6:12 l7:24 plu:24 lz:24 lj:24 lr:24"),
    ("float8_e4m3fn_x4", "eac:512 ebc:640 uc:128 uqc:1024 vc:128 wq:512 xc:384 tc:128 zc0:192 zc1:192 zc2:192 lc0:192 lc1:192 lc2:192"),
    ("uint8", "eas:512 ebs:640 us:128 uqs:1024 vs:128 wsc:512 xs:384 tsc:128 zs0:192 zs1:192 zs2:192 ls0:192 ls1:192 ls2:192"),
):
    for _w in _s.split():
        SCRATCH[_w.split(":")[0]] = ("sbuf", [128, int(_w.split(":")[1])], _d)
for _b, _s in (("kc", "fi:48 posr:48 aa:96 r2:48 r3:48 r4:48 r5:48 r6:192 r7:384 x8:16 mx4:16 mx8:16 mx8s:16 pst:16 psl:16 tmp:144 om:384 om0:96 ng:48 bm:192"),
               ("sc", "sc1:48 sc2:48 sc3:48 sc4:48 sc5:48 sc5o:48 sc6:192 sc7:384"), ("so", "so:48 so5:48 so6:192 so7:384"), ("key", "key:48 key5:48 key6:192 key7:384")):
    _o = 0
    for _w in _s.split():
        ALIAS[_w.split(":")[0]] = (_b, _o)
        _o += int(_w.split(":")[1])
    SCRATCH[_b] = ("sbuf", [128, _o], "float32")
SEMAPHORES = ["sv", "ss", "st", "sg", "ar0", "ar1", "ar2", "lsem", "dp", "dxin", "du", "dv", "dwc", "dws", "db5", "db6", "db7", "dbr", "dl", "dbo", "dbx", "dout"]


def rank_program(g, core, T, topo):
    rank = T.rank_of(core)
    if rank is None:
        return
    Q = {"v": g.vector, "s": g.scalar, "t": g.tensor, "g": g, "y": g.sync}
    SEM = {"v": "sv", "s": "ss", "t": "st", "g": "sg"}
    cnt, hist, dmh, acc = {}, {}, {}, {}
    known = {e: {} for e in Q}
    late, mode = [], {"defer": False, "mix": False}

    def hit(r, q):
        if r[2] <= q[1] or q[2] <= r[1] or r[5] <= q[4] or q[5] <= r[4]:
            return False
        return not (r[3] == q[3] and r[3] > 1 and (r[1] - q[1]) % r[3])

    def need(e, sem, val):
        k = known[e]
        if k.get(sem, 0) >= val:
            return
        Q[e].wait_ge(T.sem[sem], val)
        for s_, v_ in hist.get((sem, val), {}).items():
            k[s_] = max(k.get(s_, 0), v_)
        k[sem] = max(k.get(sem, 0), val)

    def op(e, make, writes, reads, sem=None, pre=()):
        if mode["defer"]:
            late.append((e, make, writes, reads))
            return
        own = SEM.get(e) if sem is None else None
        s = own if sem is None else sem
        todo = {}
        both = [(r, True) for r in writes] + [(r, False) for r in reads]
        for r, wr in both:
            bank = r[0] == "ps"
            for q, qw, qs, qv in acc.get(r[0], []):
                if bank and r[1] // 512 != q[1] // 512 or not bank and not hit(r, q) or not (wr or qw or bank):
                    continue
                if qs == own and (not hit(r, q) or not (wr or qw) or (e == "t" and wr)):
                    continue
                todo[qs] = max(todo.get(qs, 0), qv)
        for a_, b_ in sorted(todo.items(), key=lambda z: z[0] in dmh) + list(pre):
            if known[e].get(a_, 0) < b_:
                need(e, a_, cnt[a_] if a_ in dmh else b_)
        inc = 1 if sem is None else 16
        make().then_inc(T.sem[s], inc)
        cnt[s] = cnt.get(s, 0) + inc
        h = dict(known[e])
        if sem is not None:
            old = dmh.setdefault(s, {})
            for a_, b_ in h.items():
                old[a_] = max(old.get(a_, 0), b_)
            h = dict(old)
        h[s] = cnt[s]
        hist[(s, cnt[s])] = h
        for r, wr in both:
            keep = []
            for x in acc.get(r[0], []):
                q = x[0]
                same = q == r and (wr or (not x[1] and x[2] == s))
                if not (same or wr and r[3] == 1 and r[1] <= q[1] and q[2] <= r[2] and r[4] <= q[4] and q[5] <= r[5]):
                    keep.append(x)
            acc[r[0]] = keep + [(r, wr, s, cnt[s])]
        if e == "v" and mode["mix"] and late:
            mode["mix"] = False
            op(*late.pop(0))
            mode["mix"] = True

    def P(name, a, b, st=1, p0=0, p1=128):
        if name in ALIAS:
            name, o = ALIAS[name]
            a, b = a + o, b + o
        t, c = T[name], slice(a, b) if st == 1 else slice(a, b, st)
        ap = t[:, c] if (p0, p1) == (0, 128) else t[p0:p1, c]
        return (ap, [(name, a, b, st, p0, p1)], [])

    def IND(w, o):
        return (w[0].indirect(o[0]), w[1], o[1])

    def PS(bank, a, b, p0=0, p1=128):
        return P("ps", 512 * bank + a, 512 * bank + b, 1, p0, p1)

    def scl(s):
        return (s[0], s[1]) if isinstance(s, tuple) else (s, [])

    def tc(o, i):
        op("v", lambda: g.vector.tensor_copy(o[0], i[0]), o[1], i[1] + i[2] + o[2])

    def tt(o, i, j, k):
        op("v", lambda: g.vector.tensor_tensor(o[0], i[0], j[0], k), o[1], i[1] + i[2] + j[1])

    def ts(o, i, s1, s2, k1, k2=None):
        (a, ra), (b, rb) = scl(s1), scl(s2)
        op("v", lambda: g.vector.tensor_scalar(o[0], i[0], a, b, k1, k2) if k2 else g.vector.tensor_scalar(o[0], i[0], a, None, k1), o[1], i[1] + i[2] + ra + rb)

    def scan(o, d0, d1, init, k0, k1):
        op("v", lambda: g.vector.tensor_tensor_scan(o[0], d0[0], d1[0], init, k0, k1), o[1], d0[1] + d1[1])

    def fill(o, c):
        op("v", lambda: g.vector.memset(o[0], c), o[1], [])

    def tr(o, i):
        op("v", lambda: g.vector.transpose(o[0], i[0]), o[1], i[1])

    def quant(c, s, i):
        op("v", lambda: g.vector.quantize_mx(c[0], s[0], i[0]), c[1] + s[1], i[1])

    def act(o, i, func=F_.Copy, bias=None, scale=None):
        kw, rr = {}, []
        for n, v in (("bias", bias), ("scale", scale)):
            if v is not None:
                kw[n], ra = scl(v)
                rr = rr + ra
        op("s", lambda: g.scalar.activation(o[0], i[0], func, **kw), o[1], i[1] + i[2] + rr)

    def mm(o, l, ls, r, rs, start=True, stop=True, pre=()):
        op("t", lambda: g.tensor.matmul_mx(o[0], l[0], ls[0], r[0], rs[0], start, stop), o[1], l[1] + ls[1] + r[1] + rs[1], pre=pre)

    def dma(e, sem, o, i, wr, rd):
        op(e, lambda: Q[e].dma_start(o, i), wr, rd, sem=sem)

    def io(o, pat, base=0, cm=0, small=True):
        op("g", lambda: g.iota(o[0], pat, base, cm, allow_small_or_imprecise_dtypes=True) if small else g.iota(o[0], pat, base, cm), o[1], [])

    def sel(o, i, pat, cmp, base, cm):
        op("g", lambda: g.affine_select(o[0], i[0], pat, cmp, 0.0, base, cm), o[1], i[1])

    col = lambda k: P("cc", k, k + 1)
    BFC, SGC, S29, SSC = 0, 8, 16, 22
    PM, PM3, PM7, PM31, PMX, K6L, K7L, K5O, A6, A7, AF, Q96, O16, T0 = 30, 31, 32, 33, 34, 36, 37, 38, 40, 41, 42, 43, 44, 48
    bit = lambda b: col(BFC + b)
    sg = lambda k: col(SGC + k - 1)
    TA, TB = col(T0 + 6), col(T0 + 7)

    for q in range(8):
        dma("y", "dp", T.pin[16 * q:16 * q + 16, :], T.p[:, :], P("pin", 0, 24, 1, 16 * q, 16 * q + 16)[1], [])
    dma("s", "dxin", T.xt[:, :], T.x[:, :], P("xt", 0, 1536)[1], [])
    dma("y", "du", T.ut[:, :], T.u[:, :], P("ut", 0, 512)[1], [])
    io(P("pi", 0, 1), [[0, 1]], 0, 1, False)
    io(P("uli", 0, 64), [[16, 8], [0, 8]], small=False)
    io(P("fi", 0, 48), [[0, 3], [1, 16]])
    io(P("pst", 0, 3), [[1, 3]], 0, 3)
    io(P("ioc", 0, 384), [[1, 384]], -192)
    io(P("posr", 0, 48), [[1, 48]])
    io(P("x8", 0, 8), [[1, 8]])
    io(P("a24", 0, 24), [[32, 24]], small=False)
    ON, o6, o7 = P("on", 0, 128), P("idt", 128, 256), P("idt", 256, 384)
    fill(ON, 1.0)
    fill(P("ea", 0, 2048), 0.0)
    for b in range(4):
        sel(P("ea", 512 * b + b, 512 * b + 512, 4), ON, [[-1, 128]], A.is_equal, 0, 1)
    sel(P("idt", 0, 128), ON, [[-32, 4], [16, 2], [-1, 16]], A.is_equal, -16, 1)
    sel(o6, ON, [[-64, 2], [0, 4], [-4, 16]], A.is_ge, 0, 1)
    sel(o7, ON, [[0, 8], [-8, 16]], A.is_ge, 0, 1)
    sel(o6, o6, [[64, 2], [0, 4], [4, 16]], A.is_ge, 3, -1)
    sel(o7, o7, [[0, 8], [8, 16]], A.is_ge, 7, -1)
    for n, w, c in (("eb", 2560, 0), ("tx5", 512, 0), ("r6", 576, 0), ("tx6", 512, 0), ("m6", 291, 1), ("tx7", 512, 0), ("m7", 579, 1), ("w1", 768, 0), ("w2", 768, 0)):
        io(P(n, 0, w), [[0, w]], c)
    io(P("km", 0, 384), [[0, 2], [1, 192]])
    for b in range(7):
        ts(P("bi", b, b + 1), P("pi", 0, 1), b, 1, A.logical_shift_right, A.bitwise_and)
    for k, m in ((0, 15), (1, 3), (2, 7), (3, 31)):
        ts(P("pw", k, k + 1), P("pi", 0, 1), m, None, A.bitwise_and)
    ts(P("pw", 8, 9), P("pi", 0, 1), 4, None, A.logical_shift_right)
    for k in (1, 2, 3):
        ts(P("pw", 4 + k, 5 + k), P("pw", 0, 1), k, None, A.logical_shift_right)
    tc(P("cc", BFC, BFC + 7), P("bi", 0, 7))
    tc(P("cc", PM, PM + 4), P("pw", 0, 4))
    tc(P("ul", 0, 64), P("uli", 0, 64))
    tc(P("cc", T0, T0 + 4), P("pw", 5, 9))
    ts(P("cc", SGC, SGC + 7), P("cc", BFC, BFC + 7), -2.0, 1.0, A.mult, A.add)

    def base_out(e="odf", sem="dbo", to="bof", p=112):
        dma("y", sem, T[to][:, :], T[e][p:p + 1, :], P(to, 0, 3)[1], P(e, 0, 384)[1])

    tc(P("lp0", 0, 24), P("pin", 0, 24))
    act(P("odf", 0, 384), IND(P("ioc", 0, 384), P("lp0", 0, 24)), F_.Identity, bias=192.0)
    base_out()
    ts(P("cc", S29, S29 + 4), P("cc", SGC, SGC + 4), BIG, None, A.mult)
    tt(P("cc", SSC, SSC + 6), P("cc", SGC, SGC + 6), P("cc", SGC + 1, SGC + 7), A.mult)
    uw, uo, ul = P("uc", 0, 128), P("uqc", 0, 1024), P("ul", 0, 64)
    quant(uw, P("us", 0, 128), P("ut", 0, 512))
    tc(P("odx", 0, 384, 2), P("odf", 1, 384, 2))
    tc(P("odx", 1, 384, 2), P("odf", 0, 384, 2))
    base_out("odx", "dbx", "bxf")
    dma("y", "dwc", T.wq[:, :].bitcast(dt.uint8), T.wc[:, :], P("wq", 0, 512)[1], [])
    dma("y", "dws", T.wsc[:, :], T.ws[:, :], P("wsc", 0, 512)[1], [])
    dma("y", "dv", T.vt[:, :], T.v[:, :], P("vt", 0, 512)[1], [])
    act(P("uqs", 0, 1024), IND(P("us", 0, 128), ul))
    op("v", lambda: g.vector.tensor_copy(uo[0].bitcast(dt.uint32), uw[0].bitcast(dt.uint32).indirect(ul[0])), uo[1], uw[1] + ul[1])

    def scores_in():
        quant(P("xc", 0, 192), P("xs", 0, 192), P("xt", 0, 768))
        quant(P("xc", 192, 384), P("xs", 192, 384), P("xt", 768, 1536))

    def smm(gr, bank, a=0, b=384):
        mm(PS(bank, 0, b - a), P("uqc", 128 * gr, 128 * gr + 128), P("uqs", 128 * gr, 128 * gr + 128), P("xc", a, b), P("xs", a, b))

    def fmm(b, bank):
        mm(PS(bank, 0, 384), P("eac", 128 * b, 128 * b + 128), P("eas", 128 * b, 128 * b + 128), P("xc", 0, 384), P("xs", 0, 384))

    def xmm(k, bank, start=True, stop=True):
        mm(PS(bank, 0, 128), P("ebc", 128 * k, 128 * k + 128), P("ebs", 128 * k, 128 * k + 128), P("tc", 0, 128), P("tsc", 0, 128), start, stop)

    own = P("tmp", 0, 48)
    ts(own, P("fi", 0, 48), col(PM), None, A.is_equal)
    ts(TB, col(T0 + 3), -48.0, None, A.mult)
    ts(TA, col(PM), sg(1), None, A.add)
    fill(P("m4", 0, 147), 1.0)
    for h in (0, 48):
        ts(P("aa", h, h + 48), own, -1.0, 1.0, A.mult, A.add)
        for t in range(3):
            ts(P("om0", h + 16 * t, h + 16 * t + 16), P("tmp", 16 * t, 16 * t + 16), sg(1), 1.0 if t != 1 else -1.0, A.mult, A.mult)
    ts(P("pg", 0, 3), P("pst", 0, 3), TB, None, A.add)
    ts(P("tmp", 48, 96), P("fi", 0, 48), TA, None, A.is_equal)
    ts(P("ng", 0, 48), P("aa", 0, 48), -BIG, None, A.mult)
    fill(P("m4", 0, 147, 49), 0.0)
    ts(P("psl", 0, 3), P("pg", 0, 3), sg(1), None, A.mult)
    ts(P("bm", 0, 48), P("tmp", 48, 96), 0.0, col(S29), A.is_equal, A.mult)
    scores_in()
    mode["defer"] = True
    fill(P("r2", 0, 192), 0.0)
    for k in (2, 3, 4, 5, 6, 7):
        ts(P("om", 48 * k, 48 * k + 48), own, sg(k), None, A.mult)
    for k in (2, 3, 4):
        ts(TA, col(T0 + k - 2), sg(k), float(W[k]), A.add, A.mult)
        ts(TB, TA, float(W[k]), None, A.add)
        ts(P("tmp", 48, 96), P("posr", 0, 48), TA, None, A.is_ge)
        ts(P("tmp", 96, 144), P("posr", 0, 48), TB, None, A.is_ge)
        fill(P("r%d" % k, 0, 48, W[k]), -BIG)
        tt(P("tmp", 48, 96), P("tmp", 48, 96), P("tmp", 96, 144), A.subtract)
        ts(P("bm", 48 * k - 48, 48 * k), P("tmp", 48, 96), 0.0, col(S29 + k - 1), A.is_equal, A.mult)
    quant(P("eac", 0, 512), P("eas", 0, 512), P("ea", 0, 2048))
    for n in (5, 6, 7):
        fill(P("r%d" % n, 0, 48 if n < 6 else 2 * W[n], W[n]), -BIG)
    ts(col(Q96), col(T0 + 3), 96.0, None, A.mult)
    ts(col(O16), bit(4), 16.0, None, A.mult)
    ts(TA, bit(4), 48.0, sg(6), A.mult, A.mult)
    ts(TB, bit(5), 111.0, -103.5, A.mult, A.add)
    ts(col(K6L), TA, TB, None, A.add)
    ts(col(K5O), bit(4), 48.0, None, A.mult)
    ts(TA, sg(4), sg(6), -48.0, A.mult, A.mult)
    ts(TB, bit(2), 48.0, 48.0, A.mult, A.add)
    ts(col(A6), TA, TB, None, A.add)
    ts(P("mx4", 0, 4), P("x8", 0, 4), col(PM3), None, A.is_equal)
    ts(P("mx8", 0, 8), P("x8", 0, 8), col(PM7), None, A.is_equal)
    for k, (src, a, b, wt) in enumerate(((0, 0, 128, 1.0), (128, 0, 128, 1.0), (256, 0, 128, 1.0), (256, 96, 112, 2.0), (256, 112, 128, 2.0))):
        for d in range(2):
            ts(P("eb", 512 * k + 4 * a + d, 512 * k + 4 * b, 4), P("idt", src + a, src + b), wt if d == 0 else 1.0, None, A.mult)
    quant(P("ebc", 0, 512), P("ebs", 0, 512), P("eb", 0, 2048))
    quant(P("ebc", 512, 640), P("ebs", 512, 640), P("eb", 2048, 2560))
    for n, w in (("m6", 96), ("m7", 192)):
        fill(P(n, 0, 3 * w + 3, w + 1), 0.0)
    ts(P("mx8s", 0, 8), P("mx8", 0, 8), sg(6), None, A.mult)
    ts(TA, sg(7), 103.5, None, A.mult)
    ts(TB, bit(6), 192.0, -192.0, A.mult, A.add)
    ts(col(K7L), TA, TB, None, A.add)
    ts(TA, sg(4), sg(7), -96.0, A.mult, A.mult)
    ts(col(A7), TA, 199.5, None, A.add)
    ts(TA, bit(3), 384.0, 199.5, A.mult, A.add)
    ts(TB, bit(3), -384.0, 208.0, A.mult, A.add)
    ts(col(AF), TB, bit(4), TA, A.mult, A.add)
    tc(P("a24f", 0, 24), P("a24", 0, 24))
    tt(col(PMX), col(PM31), sg(1), A.add)
    ts(P("stl", 0, 24), P("a24f", 0, 24), col(PM31), None, A.add)
    ts(P("stl", 24, 48), P("a24f", 0, 24), col(PMX), None, A.add)
    mode["defer"], mode["mix"] = False, True

    def flush(n):
        while len(late) > n:
            op(*late.pop(0))

    SGR = lambda k: P("sgb", 384 * k, 384 * k + 384)
    EX, FIN, BF3 = 4, 5, 6
    nxt = T.cores[(rank + 1) % len(T.cores)]
    rid, pid = topo.addr(nxt)[0], topo.addr(nxt)[1]
    eng = topo.engines(core, nxt)
    half = len(eng) // 2
    mask_c, mask_s = sum(1 << e for e in eng[:half]), sum(1 << e for e in eng[half:])
    ends = lambda cn, w: P(cn, w, 3 * w + 3, w + 1)
    heads = lambda cn, w: P(cn, 0, 3 * w + 3, w + 1)

    def keys(so, key, n, res, sc, lst):
        tc(IND(P(so, 0, n), lst), P(sc, 0, n))
        scan(P(key, 0, n), P(res, 0, n), P(so, 0, n), -BIG, A.add, A.max)

    def halves(so, key, res, w):
        for h in (0, w):
            scan(P(key, h, h + w), P(res, h, h + w), P(so, h, h + w), -BIG, A.add, A.max)

    def owned(k, src):
        tt(P("bb", 0, 48), src, P("om", 48 * k, 48 * k + 48), A.mult)
        if k in (2, 3, 4):
            tt(P("mk", 0, 48), P("key", 0, 48), P("bm", 48 * k - 48, 48 * k), A.add)
        scan(P("own", 0, 48), P("aa", 0, 48), P("bb", 0, 48), 0.0, A.mult, A.add)

    def count(k, cmn, cn, mn, w, other, mine=("own", 15, 16), parts=1):
        for t in range(3):
            o = mine[1] + mine[2] * t
            ts(P(cmn, (w + 1) * t + 1, (w + 1) * t + w + 1), other, sg(k), P(mine[0], o, o + 1), A.mult, A.is_lt)
        n = (3 * w + 3) // parts
        for a in range(0, 3 * w + 3, n):
            scan(P(cn, a, a + n), P(mn, a, a + n), P(cmn, a, a + n), 0.0, A.mult, A.add)

    def lay(n, xs, tile, mask):
        for t in range(3):
            ts(P("xm", t, 3 * n, 3), P(mask, 0, n), xs[t], None, A.mult)
        ts(P(tile, 0, 12 * n, 4), P("xm", 0, 3 * n), MAG, MAG, A.add, A.subtract)
        tt(P(tile, 1, 12 * n, 4), P("xm", 0, 3 * n), P(tile, 0, 12 * n, 4), A.subtract)
        quant(P("tc", 0, 128), P("tsc", 0, 128), P(tile, 0, 512))

    pl, plo = P("pl", 0, 3), P("plo", 0, 3)
    for r in range(NR):
        last = r == NR - 1
        if r:
            scores_in()
        smm(0, 0, 0, 192)
        smm(0, 1, 192, 384)
        smm(1, 2)
        smm(2, 3)
        tc(P("lbox", 0, 3), P("bof", 0, 3))
        tc(P("lbox", 3, 6), P("bxf", 0, 3))
        tt(P("bdf", 0, 3), P("bxf", 0, 3), P("bof", 0, 3), A.subtract)
        act(P("sgb", 0, 192), PS(0, 0, 192))
        tc(P("sgb", 192, 384), PS(1, 0, 192))
        smm(3, 0)
        smm(4, 1)
        tt(P("b0", 0, 96), IND(SGR(0), P("lbox", 0, 6)), P("om0", 0, 96), A.mult)
        scan(P("own", 0, 96), P("aa", 0, 96), P("b0", 0, 96), 0.0, A.mult, A.add)
        tt(P("dd", 0, 3), P("own", 15, 48, 16), P("own", 63, 96, 16), A.is_gt)
        for t in range(3):
            ts(P("lbp", t, t + 1), P("dd", t, t + 1), P("bdf", t, t + 1), P("bof", t, t + 1), A.mult, A.add)
        lp = P("lbp", 0, 3)
        dma("y", "dbr", T.brow[0:1, 0:384], T.lbp[:, :], P("brow", 0, 384, 1, 0, 1)[1], lp[1])
        for name, n, src in (("lb5", 3, lambda q: (16 * (q + 1 - 2 * (q % 2)), 16)), ("lb6", 12, lambda q: (64 * (q // 4), 64))):
            for q in range(8):
                a, m = src(q)
                dma("y", "db" + name[2], T[name][16 * q:16 * q + 16, 0:n], T.lbp[a:a + m, 0:3], P(name, 0, n, 1, 16 * q, 16 * q + 16)[1], P("lbp", 0, 3, 1, a, a + m)[1])
        for q in range(8):
            dma("y", "db7", T.lb7[16 * q:16 * q + 16, 0:24], T.brow[0:1, 0:384], P("lb7", 0, 24, 1, 16 * q, 16 * q + 16)[1], P("brow", 0, 384, 1, 0, 1)[1])
        act(SGR(1), PS(2, 0, 384))
        act(heads("cm", 48), P("psl", 0, 3))
        smm(5, 2)
        act(SGR(2), PS(3, 0, 384))
        act(P("sc2", 0, 48), IND(SGR(2), lp))
        smm(6, 3)
        s1, b1 = P("sc1", 0, 48), P("b1", 0, 48)
        tt(s1, IND(SGR(1), lp), P("bm", 0, 48), A.add)
        tt(b1, IND(SGR(1), lp), P("ng", 0, 48), A.add)
        tt(P("sc1", 16, 32), P("sc1", 16, 32), P("sc1", 0, 16), A.max)
        scan(P("own", 0, 48), b1, b1, -BIG, A.max, A.max)
        tt(P("sc1", 32, 48), P("sc1", 32, 48), P("sc1", 16, 32), A.max)
        ts(P("os", 0, 3), P("own", 15, 48, 16), sg(1), None, A.mult)
        count(1, "cm", "c4", "m4", 48, s1, ("os", 0, 1))
        for k in (2, 3, 4):
            ts(pl, ends("c4", 48), sg(k - 1), None, A.mult)
            act(heads("cm", 48), ends("c4", 48), scale=col(SSC + k - 2))
            act(P("pg", 3 * k - 3, 3 * k), ends("c4", 48), scale=sg(k - 1))
            keys("so", "key", 48, "r%d" % k, "sc%d" % k, pl)
            owned(k, IND(P("key", 0, 48), pl))
            count(k, "cm", "c4", "m4", 48, P("mk", 0, 48))
            act(SGR(k + 1), PS(k - 2, 0, 384))
            act(P("sc%d" % (k + 1), 0, 48), IND(SGR(k + 1), lp))
            if k == 2:
                smm(7, 0)
            elif k == 3:
                fmm(0, 1)
            else:
                act(P("sc5o", 0, 48), IND(SGR(5), P("lb5", 0, 3)))
        flush(15)
        ts(P("tx5", 0, 12, 4), ends("c4", 48), MAG, MAG, A.add, A.subtract)
        tt(P("tx5", 1, 12, 4), ends("c4", 48), P("tx5", 0, 12, 4), A.subtract)
        quant(P("tc", 0, 128), P("tsc", 0, 128), P("tx5", 0, 512))
        xmm(0, EX)
        fmm(1, 2)
        act(heads("cm", 48), ends("c4", 48), scale=col(SSC + 3))
        act(P("pg", 12, 15), ends("c4", 48), scale=sg(4))
        act(SGR(6), PS(3, 0, 384))
        fmm(2, 3)
        act(P("sc6", 0, 192), IND(SGR(6), P("lb6", 0, 12)))
        act(P("fb", 0, 384), PS(1, 0, 384))
        ts(pl, ends("c4", 48), sg(4), None, A.mult)
        keys("so", "key", 48, "r5", "sc5", pl)
        ts(plo, PS(EX, 0, 3), sg(4), None, A.mult)
        tt(P("bb", 0, 48), IND(P("key", 0, 48), pl), P("om", 240, 288), A.mult)
        tc(IND(P("so5", 0, 48), plo), P("sc5o", 0, 48))
        scan(P("own", 0, 48), P("aa", 0, 48), P("bb", 0, 48), 0.0, A.mult, A.add)
        scan(P("key5", 0, 48), P("r5", 0, 48), P("so5", 0, 48), -BIG, A.add, A.max)
        count(5, "cm", "c4", "m4", 48, P("key5", 0, 48))
        flush(0)
        lay(4, [P("c4", 49 * t + 48, 49 * t + 49) for t in range(3)], "tx6", "mx4")
        xmm(1, EX)
        fmm(3, 1)
        act(heads("cm6", 96), ends("c4", 48), F_.Identity, bias=col(K6L), scale=col(SSC + 4))
        act(P("pg", 15, 18), ends("c4", 48), scale=sg(5))
        act(SGR(7), PS(0, 0, 384))
        act(P("sc7", 0, 384), IND(SGR(7), P("lb7", 0, 24)))
        act(P("fb", 384, 768), PS(2, 0, 384))
        ts(pl, ends("c4", 48), sg(5), col(K5O), A.mult, A.add)
        a = 3 if r else 0
        hm, pg, ad = P("hm", a, 18), P("pg", a, 18), P("ad", a, 18)
        ts(hm, pg, -7.5, MAG, A.add, A.add)
        ts(P("l6", 0, 12), PS(EX, 0, 12), sg(3), col(A6), A.mult, A.add)
        tc(IND(P("so6", 0, 192), P("l6", 0, 12)), P("sc6", 0, 192))
        ts(hm, hm, MAG, col(Q96), A.subtract, A.add)
        halves("so6", "key6", "r6", 96)
        tt(P("bb", 0, 48), IND(P("key6", 0, 96), pl), P("om", 288, 336), A.mult)
        tt(ad, hm, pg, A.add)
        for gr in range(a // 3, 6):
            dma("y", "dl", T.ldm[16 * gr:16 * gr + 16, 0:24], T.ad[:, 3 * gr:3 * gr + 3], P("ldm", 0, 24, 1, 16 * gr, 16 * gr + 16)[1], P("ad", 3 * gr, 3 * gr + 3)[1])
        scan(P("own", 0, 48), P("aa", 0, 48), P("bb", 0, 48), 0.0, A.mult, A.add)
        count(6, "cm6", "c6", "m6", 96, P("key6", 96, 192), parts=3)
        lay(8, [P("c6", 97 * t + 96, 97 * t + 97) for t in range(3)], "tx7", "mx8s")
        xmm(2, EX)
        xmm(3, FIN, True, False)
        act(heads("cm7", 192), ends("c6", 96), F_.Identity, bias=col(K7L), scale=col(SSC + 5))
        act(P("fb", 768, 1152), PS(3, 0, 384))
        act(P("bc", 0, 384), IND(P("ioc", 0, 384), P("lb7", 0, 24)))
        act(P("fb", 1152, 1536), PS(1, 0, 384))
        for b in range(4):
            act(P("fh", 384 * b, 384 * b + 384), P("fb", 384 * b, 384 * b + 384), scale=0.5)
        ts(pl, ends("c6", 96), sg(6), 103.5, A.mult, A.add)
        ts(P("l7", 0, 24), PS(EX, 0, 24), col(A7), None, A.add)
        tc(IND(P("so7", 0, 384), P("l7", 0, 24)), P("sc7", 0, 384))
        halves("so7", "key7", "r7", 192)
        owned(7, IND(P("key7", 0, 192), pl))
        count(7, "cm7", "c7", "m7", 192, P("key7", 192, 384), parts=3)
        x1 = [P("x1", t, t + 1) for t in range(3)]
        for t in range(3):
            ts(x1[t], P("c7", 193 * t + 192, 193 * t + 193), sg(7), -7.5, A.mult, A.add)
        lay(8, x1, "tx7", "mx8")
        xmm(4, FIN, False, True)
        ts(P("plu", 0, 24, 1, 0, 96), P("ldm", 0, 24, 1, 0, 96), P("cc", O16, O16 + 1, 1, 0, 96), None, A.add)
        ts(P("plu", 0, 24, 1, 96, 128), PS(FIN, 0, 24, 96, 128), P("cc", AF, AF + 1, 1, 96, 128), None, A.add)
        tc(IND(P("w1", 0, 768), P("plu", 0, 24)), P("bc", 0, 384))
        tr(P("t1", 0, 768), P("w1", 0, 768))
        tt(P("ow", 0, 24), P("t1", 0, 768, 32), P("t1", 16, 768, 32), A.add)
        ts(P("lz", 0, 24), P("ow", 0, 24), 192.0, None, A.add)
        tc(P("az", 0, 192), IND(P("fh", 0, 384), P("lz", 0, 12)))
        for b in range(1, 4):
            act(P("az", 192 * b, 192 * b + 192), IND(P("fb", 384 * b, 384 * b + 384), P("lz", 0, 12)), scale=0.5)
        for b in range(4):
            tt(P("zt", b, 768, 4), IND(P("fh", 384 * b, 384 * b + 384), P("lz", 12, 24)), P("az", 192 * b, 192 * b + 192), A.add)
        zc, zs = P("zc%d" % r, 0, H), P("zs%d" % r, 0, H)
        quant(zc, zs, P("zt", 0, 768))
        need("g", "sv", cnt["sv"])
        g.remote_dma(T["lc%d" % r][:, 0:H].bitcast(dt.uint8), zc[0].bitcast(dt.uint8), T.sem["ar%d" % r], T.sem.lsem, pid, rid, mask_c)
        g.remote_dma(T["ls%d" % r][:, 0:H], zs[0], T.sem["ar%d" % r], T.sem.lsem, pid, rid, mask_s)
        act(P("odf", 0, 384), IND(P("w1", 0, 768), P("stl", 0, 24)), F_.Identity, bias=192.0)
        if last:
            dma("y", "dout", T.od[:, :], T.odf[0:128:16, :], [], P("odf", 0, 384)[1])
        else:
            base_out()
            act(P("odx", 0, 384), IND(P("w1", 0, 768), P("stl", 24, 48)), F_.Identity, bias=192.0)
            base_out("odx", "dbx", "bxf")
        ts(P("h2", 0, 24), P("ow", 0, 24), 184.5, MAG, A.add, A.add)
        ts(P("h2", 0, 24), P("h2", 0, 24), MAG - 192.0, col(O16), A.subtract, A.add)
        tt(P("aj", 0, 24), P("h2", 0, 24), P("ow", 0, 24), A.add)
        tc(P("lj", 0, 24), P("aj", 0, 24))
        tc(IND(P("w2", 0, 768), P("lj", 0, 24)), P("km", 0, 384))
        tr(P("t2", 0, 768), P("w2", 0, 768))
        tt(P("iw", 0, 24), P("t2", 0, 768, 32), P("t2", 16, 768, 32), A.add)
        tc(P("lr", 0, 24), P("iw", 0, 24))
        fmm(3, BF3)
        if r == 0:
            quant(P("vc", 0, 128), P("vs", 0, 128), P("vt", 0, 512))
        pb = lambda b: P("psb", 192 * b, 192 * b + 192)
        for b in range(4):
            mm(PS(b, 0, H), P("wq", 128 * b, 128 * b + 128), P("wsc", 128 * b, 128 * b + 128), P("lc%d" % r, 0, H), P("ls%d" % r, 0, H), pre=[("ar%d" % r, 2 * half)])
        ts(pb(0), PS(0, 0, H), 0.03125, None, A.mult)
        for b in range(1, 4):
            act(pb(b), PS(b, 0, H), scale=0.03125)
        act(P("g3", 0, 384), IND(pb(3), P("lr", 0, 24)))
        for b in range(3):
            tt(P("xt", b, 1536, 4), IND(pb(b), P("lr", 0, 24)), P("fb", 384 * b, 384 * b + 384), A.add)
        tt(P("xt", 3, 1536, 4), P("g3", 0, 384), PS(BF3, 0, 384), A.add)
    scores_in()
    for h in range(2):
        a, b = 192 * h, 192 * h + 192
        q = P("xc", a, b)
        dma("y", "dout", T.oc[:, 4 * a:4 * b], q[0].bitcast(dt.uint8), [], q[1])
        mm(PS(h, 0, 192), P("vc", 0, 128), P("vs", 0, 128), q, P("xs", a, b))
        if h == 0:
            tc(P("yb", a, b), PS(h, 0, 192))
        else:
            act(P("yb", a, b), PS(h, 0, 192))
        dma("y", "dout", T.y[:, a:b], T.yb[:, a:b], [], P("yb", a, b)[1])
    for k in range(4):
        dma("y", "dout", T.osc[4 * k:4 * k + 4, :], T.xs[32 * k:32 * k + 4, :], [], P("xs", 0, 384)[1])
    g.wait_ge(T.sem.lsem, 2 * half * NR)
    for s in list(cnt):
        need("g", s, cnt[s])
